import numpy as np
import ml_dtypes


def mxq(x, axis, fmt="e4m3"):
    dtype, down = {"e4m3": (ml_dtypes.float8_e4m3fn, 7), "e5m2": (ml_dtypes.float8_e5m2, 14)}[fmt]
    v = np.moveaxis(np.asarray(x, np.float32).astype(ml_dtypes.bfloat16).astype(np.float64), axis, -1)
    blocks = v.reshape(v.shape[:-1] + (-1, 32))
    amax = np.abs(blocks).max(-1, keepdims=True)
    byte = np.maximum(np.where(amax > 0, np.frexp(amax)[1] - 1 + 127, 0) - down, 1)
    scale = np.exp2(byte - 127.0)
    codes = (blocks / scale).astype(np.float32).astype(dtype).astype(np.float64)
    return np.moveaxis((codes * scale).reshape(v.shape), -1, axis)


WIDE = False


def mx_kscale(k):
    if not WIDE:
        return np.ones(k)
    levels = np.array([10, -10, 5, -5, 0])
    if k % 512:
        return np.exp2(np.random.permutation(np.resize(levels, k // 32))).repeat(32)
    a = np.empty((k // 512, 16))
    for p in range(k // 512):
        a[p, :8] = np.random.permutation(np.resize(levels, 8))
        for g in range(8):
            far = levels[np.abs(levels - a[p, g]) >= 10]
            a[p, g + 8] = far[np.random.randint(len(far))]
    return np.exp2(a.ravel()).repeat(32)


def f64(x):
    return np.asarray(x).astype(np.float64)


def striped(idx):
    return np.tile(idx.reshape(-1, 16).T, (8, 1)).astype(np.uint16)


def unstriped(offs):
    return offs[:16].T.reshape(-1).astype(np.int64)


E2M1 = np.array([0.0, 0.5, 1.0, 1.5, 2.0, 3.0, 4.0, 6.0, -0.0, -0.5, -1.0, -1.5, -2.0, -3.0, -4.0, -6.0])


def pack_weight(w, fmt):
    k, n = w.shape
    w = f64(np.asarray(w, np.float32).astype(ml_dtypes.bfloat16)).reshape(k // 32, 32, n)
    amax = np.abs(w).max(1)
    if fmt == "e4m3":
        byte = np.frexp(amax)[1] - 1 + 127 - 7
    else:
        mant, ex = np.frexp(amax / 6.0)
        byte = np.where(mant > 0.5, ex, ex - 1) + 127
    byte = np.clip(np.where(amax > 0, byte, 1), 1, 254)
    scaled = (w * np.exp2(127.0 - byte)[:, None, :]).reshape(k, n).astype(np.float32)
    by_word = np.ascontiguousarray(scaled.reshape(k // 512, 128, 4, n).transpose(0, 1, 3, 2))
    if fmt == "e4m3":
        words = by_word.astype(ml_dtypes.float8_e4m3fn).view(np.uint8)
    else:
        c = by_word.astype(ml_dtypes.float4_e2m1fn).view(np.uint8) & 0xF
        words = (c[..., 0::2] | (c[..., 1::2] << 4)).reshape(k // 512, 128, 2 * n)
    return np.ascontiguousarray(words), np.ascontiguousarray(byte.astype(np.uint8).reshape(k // 512, 16, n))


def unpack_weight(words, scales, fmt):
    g, _, n = scales.shape
    words = np.ascontiguousarray(words).reshape(g, 128, n, -1)
    if fmt == "e4m3":
        vals = words.view(ml_dtypes.float8_e4m3fn).astype(np.float64)
    else:
        nib = np.empty((g, 128, n, 4), np.uint8)
        nib[..., 0::2] = words & 0xF
        nib[..., 1::2] = words >> 4
        vals = E2M1[nib]
    vals = vals * np.repeat(np.exp2(scales.astype(np.float64) - 127.0), 8, axis=1)[..., None]
    return vals.transpose(0, 1, 3, 2).reshape(g * 512, n)


def gelu(v):
    return 0.5 * v * (1.0 + np.tanh(np.sqrt(2.0 / np.pi) * (v + 0.044715 * v**3)))


K, T, S, P, H, N = 1536, 2048, 1024, 512, 512, 768

def setup_inputs():
    n = np.random.standard_normal
    s = mx_kscale(K)[:, None]
    u = mx_kscale(H)[:, None]
    tab_words, tab_scales = pack_weight(n((K, T)) * s, "e4m3")
    wg_words, wg_scales = pack_weight(1.5 * n((K, H)) / np.sqrt(K) / s, "e2m1")
    return {
        "tab_words": tab_words, "tab_scales": tab_scales,
        "offs": striped(np.random.permutation(T)[:S]),
        "pos1": striped(np.random.permutation(S)[:P]),
        "pos2": striped(np.random.permutation(S)[:P]),
        "w1": (2.0 * n((K, H)) / np.sqrt(K) / s).astype(np.float32),
        "wg_words": wg_words, "wg_scales": wg_scales,
        "gain": (np.exp(0.3 * n(H)) * u[:, 0]).astype(np.float32),
        "w2": (n((H, N)) / np.sqrt(H) / u).astype(np.float32),
    }

def reference(tab_words, tab_scales, offs, pos1, pos2, w1, wg_words, wg_scales, gain, w2):
    v = unpack_weight(tab_words, tab_scales, "e4m3")[:, unstriped(offs)]
    wg = unpack_weight(wg_words, wg_scales, "e2m1")
    w1q = mxq(f64(w1), 0, "e4m3")
    c = w1q.T @ v
    g = wg.T @ v
    h = c * (1.0 / (1.0 + np.exp(-g)))
    a = h[:, unstriped(pos1)]
    b = h[:, unstriped(pos2)]
    z = f64(gain)[:, None] * (a * np.tanh(b))
    zq = mxq(z, 0, "e4m3")
    w2q = mxq(f64(w2), 0, "e4m3")
    return w2q.T @ zq

@@ -1,0 +1,260 @@
+from contextlib import ExitStack
+
+import concourse.mybir as mybir
+
+K, T, S, PAIRS, H, N = 1536, 2048, 1024, 512, 512, 768
+FLOPS = 2 * (2 * K * H * S + H * N * PAIRS)
+
+F32 = mybir.dt.float32
+BF16 = mybir.dt.bfloat16
+I32 = mybir.dt.int32
+U32 = mybir.dt.uint32
+U16 = mybir.dt.uint16
+U8 = mybir.dt.uint8
+FP8X4 = mybir.dt.float8_e4m3fn_x4
+FP4X4 = mybir.dt.float4_e2m1fn_x4
+MULT = mybir.AluOpType.mult
+ACT = mybir.ActivationFunctionType
+
+P = 128
+PACK = 4
+PASSES = K // (P * PACK)
+BANK = 512
+HALF = PAIRS // 2
+
+
+def tile_list_fused_passage_pairs_kernel(
+    tc, tab_words, tab_scales, offs, pos1, pos2, w1, wg_words, wg_scales, gain, w2, out
+):
+    nc = tc.nc
+    with ExitStack() as ctx:
+        keep = ctx.enter_context(tc.tile_pool(name="keep", bufs=1))
+        psum = ctx.enter_context(tc.psum_pool(name="psum", bufs=4))
+
+        def sb(name, shape, dtype):
+            return keep.tile(shape, dtype, name=name, align_bytes=64)
+
+        offs_sb = keep.tile([P, S // 16], U16, name="offs_sb")
+        pos1_sb = keep.tile([P, PAIRS // 16], U16, name="pos1_sb")
+        pos2_sb = keep.tile([P, PAIRS // 16], U16, name="pos2_sb")
+
+        scale_rows = sb("scale_rows", [P, T], U8)
+        wg_scale_raw = sb("wg_scale_raw", [P, PASSES * H], U8)
+        v_planes = sb("v_planes", [P, PASSES * S], U8)
+        nc.vector.memset(scale_rows[:].bitcast(I32), 0)
+        nc.vector.memset(wg_scale_raw[:].bitcast(I32), 0)
+        nc.vector.memset(v_planes[:].bitcast(I32), 0)
+
+        nc.sync.dma_start(offs_sb[:], offs)
+        table = [sb("table%d" % a, [P, T], U32) for a in range(PASSES)]
+        for a in range(PASSES):
+            nc.gpsimd.dma_start(
+                out=scale_rows[a : 16 * PASSES : PASSES, :].bitcast(I32), in_=tab_scales[a].bitcast(I32)
+            )
+        for a in range(PASSES):
+            nc.sync.dma_start(
+                out=table[a][:].bitcast(I32),
+                in_=tab_words[a].rearrange("p t i -> p (t i)").bitcast(I32),
+            )
+        wg_raw = sb("wg_raw", [P, PASSES, H // 2], I32)
+        nc.sync.dma_start(out=wg_raw[:], in_=wg_words.bitcast(I32).rearrange("a p e -> p a e"))
+        for q in range(4):
+            nc.gpsimd.dma_start(
+                out=wg_scale_raw[32 * q : 32 * q + 4, :].bitcast(I32).rearrange("r (a e) -> r a e", a=PASSES),
+                in_=wg_scales.bitcast(I32)[:, 4 * q : 4 * q + 4, :].rearrange("a r e -> r a e"),
+            )
+        w1_raw = [sb("w1_raw%d" % a, [P, PACK, H], F32) for a in range(PASSES)]
+        for a in range(PASSES):
+            nc.sync.dma_start(
+                out=w1_raw[a][:],
+                in_=w1[512 * a : 512 * (a + 1), :].rearrange("(p j) c -> p j c", j=PACK),
+            )
+        nc.sync.dma_start(pos2_sb[:], pos2)
+        nc.sync.dma_start(pos1_sb[:], pos1)
+        gain_sb = [sb("gain%d" % t, [P, 1], F32) for t in range(PACK)]
+        gain_rows = gain.rearrange("(b t i o) -> t b i o", t=PACK, i=8, o=1)
+        with nc.allow_non_contiguous_dma(reason="one gain to a partition"):
+            for t in range(PACK):
+                nc.sync.dma_start(out=gain_sb[t][:], in_=gain_rows[t])
+        w2_raw = sb("w2_raw", [P, PACK, N], F32)
+        w2_rows = w2.rearrange("(b t i) n -> t b i n", t=PACK, i=8)
+        for t in range(PACK):
+            nc.sync.dma_start(out=w2_raw[:, t, :], in_=w2_rows[t])
+
+        picked_rows = sb("picked_rows", [P, S], U8)
+        nc.vector.tensor_copy(picked_rows[:], scale_rows[:].indirect(offs_sb[:]))
+        for q in range(4):
+            nc.gpsimd.dma_start(
+                out=v_planes[32 * q : 32 * q + 4, :].bitcast(I32).rearrange("r (a s) -> r a s", a=PASSES),
+                in_=picked_rows[12 * q : 12 * q + 12, :].bitcast(I32),
+            )
+        v_words = [sb("v_words%d" % a, [P, S], U32) for a in range(PASSES)]
+        for a in range(PASSES):
+            nc.vector.tensor_copy(v_words[a][:], table[a][:].indirect(offs_sb[:]))
+
+        wg_codes = sb("wg_codes", [P, PASSES * 2 * H], U8)
+        wg_planes = sb("wg_planes", [P, PASSES * H], U8)
+        nc.vector.tensor_copy(
+            out=wg_codes[:].bitcast(I32).rearrange("p (a t b i) -> p a t b i", a=PASSES, t=PACK, i=4),
+            in_=wg_raw[:].rearrange("p a (b t i) -> p a t b i", t=PACK, i=4),
+        )
+        nc.vector.tensor_copy(
+            out=wg_planes[:].bitcast(I32).rearrange("p (a t b i) -> p a t b i", a=PASSES, t=PACK, i=2),
+            in_=wg_scale_raw[:].bitcast(I32).rearrange("p (a b t i) -> p a t b i", a=PASSES, t=PACK, i=2),
+        )
+
+        gates = [sb("gate%d" % t, [P, S], F32) for t in range(PACK)]
+
+        def make_gate(t):
+            for u in range(S // BANK):
+                acc = psum.tile([P, BANK], F32, name="g_acc")
+                for a in range(PASSES):
+                    col = a * H + t * P
+                    nc.tensor.matmul_mx(
+                        out=acc[:],
+                        lhsT=wg_codes[:, 2 * col : 2 * (col + P)].bitcast(FP4X4),
+                        lhsT_scale=wg_planes[:, col : col + P],
+                        rhs=v_words[a][:, u * BANK : (u + 1) * BANK].bitcast(FP8X4),
+                        rhs_scale=v_planes[:, a * S + u * BANK : a * S + (u + 1) * BANK],
+                        start=(a == 0),
+                        stop=(a == PASSES - 1),
+                    )
+                nc.scalar.activation(gates[t][:, u * BANK : (u + 1) * BANK], acc[:], ACT.Sigmoid)
+
+        w1_bf = [sb("w1_bf%d" % a, [P, PACK * H], BF16) for a in range(PASSES)]
+        w1_codes = [sb("w1_codes%d" % a, [P, H], U32) for a in range(PASSES)]
+        w1_planes = [sb("w1_planes%d" % a, [P, H], U8) for a in range(PASSES)]
+
+        def cast_w1(a, t):
+            nc.vector.tensor_copy(
+                out=w1_bf[a][:, t * H : (t + 1) * H].rearrange("p (b h i j) -> p b h j i", h=2, i=4, j=PACK),
+                in_=w1_raw[a][:].rearrange("p j (b t h i) -> p t b h j i", t=PACK, h=2, i=4)[:, t],
+            )
+
+        def quantise_w1(a, t0, t1):
+            nc.vector.quantize_mx(
+                out=w1_codes[a][:, t0 * P : t1 * P].bitcast(FP8X4),
+                scales=w1_planes[a][:, t0 * P : t1 * P],
+                in_=w1_bf[a][:, t0 * H : t1 * H],
+            )
+
+        for a in range(PASSES - 1):
+            for t in range(PACK):
+                cast_w1(a, t)
+            quantise_w1(a, 0, PACK)
+        last = PASSES - 1
+        cast_w1(last, 0)
+        for t in range(PACK):
+            if t + 1 < PACK:
+                cast_w1(last, t + 1)
+            quantise_w1(last, t, t + 1)
+
+        w2_bf = sb("w2_bf", [P, N * PACK], BF16)
+        w2_codes = sb("w2_codes", [P, N], U32)
+        w2_planes = sb("w2_planes", [P, N], U8)
+
+        def cast_w2(m):
+            nc.scalar.copy(
+                out=w2_bf[:, m * P * PACK : (m + 1) * P * PACK].rearrange("p (c i t) -> p c t i", i=4, t=PACK),
+                in_=w2_raw[:, :, m * P : (m + 1) * P].rearrange("p t (c i) -> p c t i", i=4),
+            )
+
+        def quantise_w2(m0, m1):
+            nc.vector.quantize_mx(
+                out=w2_codes[:, m0 * P : m1 * P].bitcast(FP8X4),
+                scales=w2_planes[:, m0 * P : m1 * P],
+                in_=w2_bf[:, m0 * P * PACK : m1 * P * PACK],
+            )
+
+        h = [sb("h%d" % t, [P, S], F32) for t in range(PACK)]
+        second = [sb("second%d" % e, [P, PACK, HALF], F32) for e in range(2)]
+        bent = [sb("bent%d" % e, [P, PACK, HALF], F32) for e in range(2)]
+        factor = [sb("factor%d" % e, [P, PACK, HALF], F32) for e in range(2)]
+        z = [sb("z%d" % e, [P, PACK, HALF], F32) for e in range(2)]
+        z_bf = [sb("z_bf%d" % e, [P, HALF * PACK], BF16) for e in range(2)]
+        z_codes = [sb("z_codes%d" % e, [P, HALF], U32) for e in range(2)]
+        z_planes = [sb("z_planes%d" % e, [P, HALF], U8) for e in range(2)]
+        cols = HALF // 16
+
+        def make_h(t):
+            for u in range(S // BANK):
+                acc = psum.tile([P, BANK], F32, name="c_acc")
+                for a in range(PASSES):
+                    nc.tensor.matmul_mx(
+                        out=acc[:],
+                        lhsT=w1_codes[a][:, t * P : (t + 1) * P].bitcast(FP8X4),
+                        lhsT_scale=w1_planes[a][:, t * P : (t + 1) * P],
+                        rhs=v_words[a][:, u * BANK : (u + 1) * BANK].bitcast(FP8X4),
+                        rhs_scale=v_planes[:, a * S + u * BANK : a * S + (u + 1) * BANK],
+                        start=(a == 0),
+                        stop=(a == PASSES - 1),
+                    )
+                span = slice(u * BANK, (u + 1) * BANK)
+                nc.vector.tensor_tensor(h[t][:, span], acc[:], gates[t][:, span], MULT)
+
+        def pick_second(e, t):
+            nc.vector.tensor_copy(second[e][:, t, :], h[t][:].indirect(pos2_sb[:, e * cols : (e + 1) * cols]))
+            nc.scalar.activation(bent[e][:, t, :], second[e][:, t, :], ACT.Tanh)
+            nc.scalar.activation(factor[e][:, t, :], bent[e][:, t, :], ACT.Copy, scale=gain_sb[t][:])
+
+        def pick_first(e, t):
+            nc.vector.tensor_tensor(
+                z[e][:, t, :], h[t][:].indirect(pos1_sb[:, e * cols : (e + 1) * cols]), factor[e][:, t, :], MULT
+            )
+
+        def weave(e, copy):
+            copy(
+                out=z_bf[e][:].rearrange("p (c i t) -> p c t i", i=4, t=PACK),
+                in_=z[e][:].rearrange("p t (c i) -> p c t i", i=4),
+            )
+
+        def quantise_z(e):
+            nc.vector.quantize_mx(out=z_codes[e][:].bitcast(FP8X4), scales=z_planes[e][:], in_=z_bf[e][:])
+
+        def project(e, copies):
+            for g in range(N // (2 * P)):
+                acc = psum.tile([P, BANK], F32, name="g_acc")
+                for s in range(2):
+                    m = 2 * g + s
+                    nc.tensor.matmul_mx(
+                        out=acc[:, s * HALF : (s + 1) * HALF],
+                        lhsT=w2_codes[:, m * P : (m + 1) * P].bitcast(FP8X4),
+                        lhsT_scale=w2_planes[:, m * P : (m + 1) * P],
+                        rhs=z_codes[e][:].bitcast(FP8X4),
+                        rhs_scale=z_planes[e][:],
+                        start=True,
+                        stop=True,
+                    )
+                res = sb("res%d_%d" % (e, g), [P, BANK], F32)
+                copies[g](out=res[:], in_=acc[:])
+                nc.sync.dma_start(
+                    out=out[2 * g * P : 2 * (g + 1) * P, e * HALF : (e + 1) * HALF].rearrange("(s p) j -> p s j", p=P),
+                    in_=res[:].rearrange("p (s j) -> p s j", s=2),
+                )
+
+        for t in range(PACK):
+            make_gate(t)
+            make_h(t)
+            pick_second(0, t)
+            if t > 0:
+                pick_first(0, t - 1)
+            if t < 3:
+                cast_w2(2 * t)
+                cast_w2(2 * t + 1)
+        pick_second(1, 0)
+        pick_first(0, PACK - 1)
+        weave(0, nc.scalar.copy)
+        quantise_w2(0, 4)
+        quantise_w2(4, 6)
+        pick_second(1, 1)
+        pick_first(1, 0)
+        quantise_z(0)
+        project(0, [nc.scalar.copy] * 3)
+        pick_second(1, 2)
+        pick_first(1, 1)
+        pick_second(1, 3)
+        pick_first(1, 2)
+        pick_first(1, 3)
+        weave(1, nc.vector.tensor_copy)
+        quantise_z(1)
+        project(1, [nc.scalar.copy, nc.vector.tensor_copy, nc.scalar.copy])

@@ -46,31 +46,36 @@ def tile_list_fused_passage_pairs_kernel(
         nc.vector.memset(v_planes[:].bitcast(I32), 0)
 
         nc.sync.dma_start(offs_sb[:], offs)
+        nc.sync.dma_start(pos2_sb[:], pos2)
+        nc.sync.dma_start(pos1_sb[:], pos1)
+        wg_raw = sb("wg_raw", [P, PASSES, H // 2], I32)
+        nc.sync.dma_start(out=wg_raw[:], in_=wg_words.bitcast(I32).rearrange("a p e -> p a e"))
         table = [sb("table%d" % a, [P, T], U32) for a in range(PASSES)]
         for a in range(PASSES):
-            nc.gpsimd.dma_start(
+            nc.sync.dma_start(
                 out=scale_rows[a : 16 * PASSES : PASSES, :].bitcast(I32), in_=tab_scales[a].bitcast(I32)
             )
-        for a in range(PASSES):
+
+        def load_table(a):
             nc.sync.dma_start(
                 out=table[a][:].bitcast(I32),
                 in_=tab_words[a].rearrange("p t i -> p (t i)").bitcast(I32),
             )
-        wg_raw = sb("wg_raw", [P, PASSES, H // 2], I32)
-        nc.sync.dma_start(out=wg_raw[:], in_=wg_words.bitcast(I32).rearrange("a p e -> p a e"))
+
+        load_table(0)
         for q in range(4):
-            nc.gpsimd.dma_start(
+            nc.sync.dma_start(
                 out=wg_scale_raw[32 * q : 32 * q + 4, :].bitcast(I32).rearrange("r (a e) -> r a e", a=PASSES),
                 in_=wg_scales.bitcast(I32)[:, 4 * q : 4 * q + 4, :].rearrange("a r e -> r a e"),
             )
-        w1_raw = [sb("w1_raw%d" % a, [P, PACK, H], F32) for a in range(PASSES)]
+        load_table(1)
+        load_table(2)
+        w1_raw = [keep.tile([P, PACK, H], F32, name="w1_raw%d" % a, tag="slot%d" % a, align_bytes=64) for a in range(PASSES)]
         for a in range(PASSES):
             nc.sync.dma_start(
                 out=w1_raw[a][:],
                 in_=w1[512 * a : 512 * (a + 1), :].rearrange("(p j) c -> p j c", j=PACK),
             )
-        nc.sync.dma_start(pos2_sb[:], pos2)
-        nc.sync.dma_start(pos1_sb[:], pos1)
         gain_sb = [sb("gain%d" % t, [P, 1], F32) for t in range(PACK)]
         gain_rows = gain.rearrange("(b t i o) -> t b i o", t=PACK, i=8, o=1)
         with nc.allow_non_contiguous_dma(reason="one gain to a partition"):
@@ -84,7 +89,7 @@ def tile_list_fused_passage_pairs_kernel(
         picked_rows = sb("picked_rows", [P, S], U8)
         nc.vector.tensor_copy(picked_rows[:], scale_rows[:].indirect(offs_sb[:]))
         for q in range(4):
-            nc.gpsimd.dma_start(
+            nc.scalar.dma_start(
                 out=v_planes[32 * q : 32 * q + 4, :].bitcast(I32).rearrange("r (a s) -> r a s", a=PASSES),
                 in_=picked_rows[12 * q : 12 * q + 12, :].bitcast(I32),
             )
@@ -103,7 +108,36 @@ def tile_list_fused_passage_pairs_kernel(
             in_=wg_scale_raw[:].bitcast(I32).rearrange("p (a b t i) -> p a t b i", a=PASSES, t=PACK, i=2),
         )
 
-        gates = [sb("gate%d" % t, [P, S], F32) for t in range(PACK)]
+        w1_bf = [sb("w1_bf%d" % a, [P, PACK * H], BF16) for a in range(PASSES)]
+        w1_codes = [sb("w1_codes%d" % a, [P, H], U32) for a in range(PASSES)]
+        w1_planes = [sb("w1_planes%d" % a, [P, H], U8) for a in range(PASSES)]
+
+        def cast_w1(a, t, copy):
+            copy(
+                out=w1_bf[a][:, t * H : (t + 1) * H].rearrange("p (b h i j) -> p b h j i", h=2, i=4, j=PACK),
+                in_=w1_raw[a][:].rearrange("p j (b t h i) -> p t b h j i", t=PACK, h=2, i=4)[:, t],
+            )
+
+        def quantise_w1(a, t0, t1):
+            nc.vector.quantize_mx(
+                out=w1_codes[a][:, t0 * P : t1 * P].bitcast(FP8X4),
+                scales=w1_planes[a][:, t0 * P : t1 * P],
+                in_=w1_bf[a][:, t0 * H : t1 * H],
+            )
+
+        for a in range(PASSES - 1):
+            for t in range(PACK):
+                cast_w1(a, t, nc.scalar.copy if a == 0 else nc.vector.tensor_copy)
+            quantise_w1(a, 0, PACK)
+        last = PASSES - 1
+        cast_w1(last, 0, nc.vector.tensor_copy)
+        for t in range(PACK):
+            if t + 1 < PACK:
+                cast_w1(last, t + 1, nc.scalar.copy)
+            quantise_w1(last, t, t + 1)
+
+        gate_pairs = [keep.tile([P, 2, S], F32, name="gates%d" % a, tag="slot%d" % a, align_bytes=64) for a in range(2)]
+        gates = [gate_pairs[t // 2][:, t % 2, :] for t in range(PACK)]
 
         def make_gate(t):
             for u in range(S // BANK):
@@ -120,34 +154,6 @@ def tile_list_fused_passage_pairs_kernel(
                         stop=(a == PASSES - 1),
                     )
                 nc.scalar.activation(gates[t][:, u * BANK : (u + 1) * BANK], acc[:], ACT.Sigmoid)
-
-        w1_bf = [sb("w1_bf%d" % a, [P, PACK * H], BF16) for a in range(PASSES)]
-        w1_codes = [sb("w1_codes%d" % a, [P, H], U32) for a in range(PASSES)]
-        w1_planes = [sb("w1_planes%d" % a, [P, H], U8) for a in range(PASSES)]
-
-        def cast_w1(a, t):
-            nc.vector.tensor_copy(
-                out=w1_bf[a][:, t * H : (t + 1) * H].rearrange("p (b h i j) -> p b h j i", h=2, i=4, j=PACK),
-                in_=w1_raw[a][:].rearrange("p j (b t h i) -> p t b h j i", t=PACK, h=2, i=4)[:, t],
-            )
-
-        def quantise_w1(a, t0, t1):
-            nc.vector.quantize_mx(
-                out=w1_codes[a][:, t0 * P : t1 * P].bitcast(FP8X4),
-                scales=w1_planes[a][:, t0 * P : t1 * P],
-                in_=w1_bf[a][:, t0 * H : t1 * H],
-            )
-
-        for a in range(PASSES - 1):
-            for t in range(PACK):
-                cast_w1(a, t)
-            quantise_w1(a, 0, PACK)
-        last = PASSES - 1
-        cast_w1(last, 0)
-        for t in range(PACK):
-            if t + 1 < PACK:
-                cast_w1(last, t + 1)
-            quantise_w1(last, t, t + 1)
 
         w2_bf = sb("w2_bf", [P, N * PACK], BF16)
         w2_codes = sb("w2_codes", [P, N], U32)
@@ -167,7 +173,7 @@ def tile_list_fused_passage_pairs_kernel(
             )
 
         h = [sb("h%d" % t, [P, S], F32) for t in range(PACK)]
-        second = [sb("second%d" % e, [P, PACK, HALF], F32) for e in range(2)]
+        second = [keep.tile([P, PACK, HALF], F32, name="second0", tag="second", align_bytes=64)]
         bent = [sb("bent%d" % e, [P, PACK, HALF], F32) for e in range(2)]
         factor = [sb("factor%d" % e, [P, PACK, HALF], F32) for e in range(2)]
         z = [sb("z%d" % e, [P, PACK, HALF], F32) for e in range(2)]
@@ -241,6 +247,7 @@ def tile_list_fused_passage_pairs_kernel(
             if t < 3:
                 cast_w2(2 * t)
                 cast_w2(2 * t + 1)
+        second.append(keep.tile([P, PACK, HALF], F32, name="second1", tag="second", align_bytes=64))
         pick_second(1, 0)
         pick_first(0, PACK - 1)
         weave(0, nc.scalar.copy)

@@ -29,6 +29,7 @@ def tile_list_fused_passage_pairs_kernel(
     nc = tc.nc
     with ExitStack() as ctx:
         keep = ctx.enter_context(tc.tile_pool(name="keep", bufs=1))
+        shared = ctx.enter_context(tc.tile_pool(name="shared", bufs=1))
         psum = ctx.enter_context(tc.psum_pool(name="psum", bufs=4))
 
         def sb(name, shape, dtype):
@@ -38,23 +39,35 @@ def tile_list_fused_passage_pairs_kernel(
         pos1_sb = keep.tile([P, PAIRS // 16], U16, name="pos1_sb")
         pos2_sb = keep.tile([P, PAIRS // 16], U16, name="pos2_sb")
 
-        scale_rows = sb("scale_rows", [P, T], U8)
+        def slot(name, shape, dtype, n):
+            return keep.tile(shape, dtype, name=name, tag="slot%d" % n, align_bytes=64)
+
+        scale_rows = shared.tile([P, T], U8, name="scale_rows", offset=4096, align_bytes=64)
         wg_scale_raw = sb("wg_scale_raw", [P, PASSES * H], U8)
         v_planes = sb("v_planes", [P, PASSES * S], U8)
         nc.vector.memset(scale_rows[:].bitcast(I32), 0)
-        nc.vector.memset(wg_scale_raw[:].bitcast(I32), 0)
         nc.vector.memset(v_planes[:].bitcast(I32), 0)
+
+        warm = sb("warm", [P, 2], F32)
+        nc.gpsimd.memset(warm[:, 0:1], 0.0)
+        nc.scalar.activation(warm[:, 1:2], warm[:, 0:1], ACT.Sigmoid)
+        wg_planes = sb("wg_planes", [P, PASSES * H], U8)
+        nc.gpsimd.memset(wg_planes[:].bitcast(I32), 0)
 
         nc.sync.dma_start(offs_sb[:], offs)
         nc.sync.dma_start(pos2_sb[:], pos2)
         nc.sync.dma_start(pos1_sb[:], pos1)
-        wg_raw = sb("wg_raw", [P, PASSES, H // 2], I32)
-        nc.sync.dma_start(out=wg_raw[:], in_=wg_words.bitcast(I32).rearrange("a p e -> p a e"))
-        table = [sb("table%d" % a, [P, T], U32) for a in range(PASSES)]
-        for a in range(PASSES):
+        gain_sb = [sb("gain%d" % t, [P, 1], F32) for t in range(PACK)]
+        gain_rows = gain.rearrange("(b t i o) -> t b i o", t=PACK, i=8, o=1)
+        with nc.allow_non_contiguous_dma(reason="one gain to a partition"):
+            for t in range(PACK):
+                nc.gpsimd.dma_start(out=gain_sb[t][:], in_=gain_rows[t])
+        for q in range(4):
             nc.sync.dma_start(
-                out=scale_rows[a : 16 * PASSES : PASSES, :].bitcast(I32), in_=tab_scales[a].bitcast(I32)
+                out=wg_scale_raw[32 * q : 32 * q + 4, :].bitcast(I32).rearrange("r (a e) -> r a e", a=PASSES),
+                in_=wg_scales.bitcast(I32)[:, 4 * q : 4 * q + 4, :].rearrange("a r e -> r a e"),
             )
+        table = [slot("table%d" % a, [P, T], U32, a) for a in range(PASSES)]
 
         def load_table(a):
             nc.sync.dma_start(
@@ -63,53 +76,52 @@ def tile_list_fused_passage_pairs_kernel(
             )
 
         load_table(0)
-        for q in range(4):
-            nc.sync.dma_start(
-                out=wg_scale_raw[32 * q : 32 * q + 4, :].bitcast(I32).rearrange("r (a e) -> r a e", a=PASSES),
-                in_=wg_scales.bitcast(I32)[:, 4 * q : 4 * q + 4, :].rearrange("a r e -> r a e"),
-            )
+        nc.sync.dma_start(
+            out=scale_rows[0 : 16 * PASSES, :].bitcast(I32), in_=tab_scales.bitcast(I32).rearrange("a q t -> q a t")
+        )
+        wg_raw = sb("wg_raw", [P, PASSES, H // 2], I32)
+        nc.sync.dma_start(out=wg_raw[:], in_=wg_words.bitcast(I32).rearrange("a p e -> p a e"))
         load_table(1)
         load_table(2)
-        w1_raw = [keep.tile([P, PACK, H], F32, name="w1_raw%d" % a, tag="slot%d" % a, align_bytes=64) for a in range(PASSES)]
+
+        picked_rows = sb("picked_rows", [P, S], U8)
+        nc.vector.tensor_copy(picked_rows[:], scale_rows[:].indirect(offs_sb[:]))
+        for q in range(4):
+            (nc.sync if q % 2 else nc.scalar).dma_start(
+                out=v_planes[32 * q : 32 * q + 4, :].bitcast(I32).rearrange("r (a s) -> r a s", a=PASSES),
+                in_=picked_rows[12 * q : 12 * q + 12, :].bitcast(I32),
+            )
+        v_words = [shared.tile([P, S], U32, name="v_words0", offset=1024, align_bytes=64)]
+        v_words.extend(sb("v_words%d" % a, [P, S], U32) for a in range(1, PASSES))
+        for a in range(PASSES):
+            nc.vector.tensor_copy(v_words[a][:], table[a][:].indirect(offs_sb[:]))
+
+        w1_raw = [shared.tile([P, PACK, H], F32, name="w1_raw0", offset=5120, align_bytes=64)]
+        w1_raw.extend(slot("w1_raw%d" % a, [P, PACK, H], F32, a - 1) for a in range(1, PASSES))
         for a in range(PASSES):
             nc.sync.dma_start(
                 out=w1_raw[a][:],
                 in_=w1[512 * a : 512 * (a + 1), :].rearrange("(p j) c -> p j c", j=PACK),
             )
-        gain_sb = [sb("gain%d" % t, [P, 1], F32) for t in range(PACK)]
-        gain_rows = gain.rearrange("(b t i o) -> t b i o", t=PACK, i=8, o=1)
-        with nc.allow_non_contiguous_dma(reason="one gain to a partition"):
-            for t in range(PACK):
-                nc.sync.dma_start(out=gain_sb[t][:], in_=gain_rows[t])
-        w2_raw = sb("w2_raw", [P, PACK, N], F32)
+        w2_raw = slot("w2_raw", [P, PACK, N], F32, 2)
         w2_rows = w2.rearrange("(b t i) n -> t b i n", t=PACK, i=8)
         for t in range(PACK):
             nc.sync.dma_start(out=w2_raw[:, t, :], in_=w2_rows[t])
 
-        picked_rows = sb("picked_rows", [P, S], U8)
-        nc.vector.tensor_copy(picked_rows[:], scale_rows[:].indirect(offs_sb[:]))
-        for q in range(4):
-            nc.scalar.dma_start(
-                out=v_planes[32 * q : 32 * q + 4, :].bitcast(I32).rearrange("r (a s) -> r a s", a=PASSES),
-                in_=picked_rows[12 * q : 12 * q + 12, :].bitcast(I32),
-            )
-        v_words = [sb("v_words%d" % a, [P, S], U32) for a in range(PASSES)]
-        for a in range(PASSES):
-            nc.vector.tensor_copy(v_words[a][:], table[a][:].indirect(offs_sb[:]))
-
         wg_codes = sb("wg_codes", [P, PASSES * 2 * H], U8)
-        wg_planes = sb("wg_planes", [P, PASSES * H], U8)
         nc.vector.tensor_copy(
             out=wg_codes[:].bitcast(I32).rearrange("p (a t b i) -> p a t b i", a=PASSES, t=PACK, i=4),
             in_=wg_raw[:].rearrange("p a (b t i) -> p a t b i", t=PACK, i=4),
         )
-        nc.vector.tensor_copy(
-            out=wg_planes[:].bitcast(I32).rearrange("p (a t b i) -> p a t b i", a=PASSES, t=PACK, i=2),
-            in_=wg_scale_raw[:].bitcast(I32).rearrange("p (a b t i) -> p a t b i", a=PASSES, t=PACK, i=2),
-        )
+        for q in range(4):
+            live = slice(32 * q, 32 * q + 4)
+            nc.vector.tensor_copy(
+                out=wg_planes[live, :].bitcast(I32).rearrange("p (a t b i) -> p a t b i", a=PASSES, t=PACK, i=2),
+                in_=wg_scale_raw[live, :].bitcast(I32).rearrange("p (a b t i) -> p a t b i", a=PASSES, t=PACK, i=2),
+            )
 
         w1_bf = [sb("w1_bf%d" % a, [P, PACK * H], BF16) for a in range(PASSES)]
-        w1_codes = [sb("w1_codes%d" % a, [P, H], U32) for a in range(PASSES)]
+        w1_codes = [keep.tile([P, H], U32, name="w1_codes%d" % a, tag="codes%d" % a, align_bytes=64) for a in range(PASSES)]
         w1_planes = [sb("w1_planes%d" % a, [P, H], U8) for a in range(PASSES)]
 
         def cast_w1(a, t, copy):
@@ -136,27 +148,38 @@ def tile_list_fused_passage_pairs_kernel(
                 cast_w1(last, t + 1, nc.scalar.copy)
             quantise_w1(last, t, t + 1)
 
-        gate_pairs = [keep.tile([P, 2, S], F32, name="gates%d" % a, tag="slot%d" % a, align_bytes=64) for a in range(2)]
-        gates = [gate_pairs[t // 2][:, t % 2, :] for t in range(PACK)]
+        rows = shared.tile([P, PACK + 1, S], F32, name="rows", offset=5120, align_bytes=64)
+        gates = [rows[:, t, :] for t in range(PACK)]
 
-        def make_gate(t):
-            for u in range(S // BANK):
-                acc = psum.tile([P, BANK], F32, name="g_acc")
-                for a in range(PASSES):
-                    col = a * H + t * P
+        def product(slices, tag, stationary):
+            groups = [(t, u) for t in slices for u in range(S // BANK)]
+            accs = [psum.tile([P, BANK], F32, name=tag) for group in groups]
+            for a in range(PASSES):
+                for (t, u), acc in zip(groups, accs):
+                    codes, planes = stationary(a, t)
                     nc.tensor.matmul_mx(
                         out=acc[:],
-                        lhsT=wg_codes[:, 2 * col : 2 * (col + P)].bitcast(FP4X4),
-                        lhsT_scale=wg_planes[:, col : col + P],
+                        lhsT=codes,
+                        lhsT_scale=planes,
                         rhs=v_words[a][:, u * BANK : (u + 1) * BANK].bitcast(FP8X4),
                         rhs_scale=v_planes[:, a * S + u * BANK : a * S + (u + 1) * BANK],
                         start=(a == 0),
                         stop=(a == PASSES - 1),
                     )
+            return zip(groups, accs)
+
+        def wg_slice(a, t):
+            col = a * H + t * P
+            return wg_codes[:, 2 * col : 2 * (col + P)].bitcast(FP4X4), wg_planes[:, col : col + P]
+
+        def w1_slice(a, t):
+            return w1_codes[a][:, t * P : (t + 1) * P].bitcast(FP8X4), w1_planes[a][:, t * P : (t + 1) * P]
+
+        def make_gates(slices):
+            for (t, u), acc in product(slices, "g_acc", wg_slice):
                 nc.scalar.activation(gates[t][:, u * BANK : (u + 1) * BANK], acc[:], ACT.Sigmoid)
 
         w2_bf = sb("w2_bf", [P, N * PACK], BF16)
-        w2_codes = sb("w2_codes", [P, N], U32)
         w2_planes = sb("w2_planes", [P, N], U8)
 
         def cast_w2(m):
@@ -165,53 +188,42 @@ def tile_list_fused_passage_pairs_kernel(
                 in_=w2_raw[:, :, m * P : (m + 1) * P].rearrange("p t (c i) -> p c t i", i=4),
             )
 
-        def quantise_w2(m0, m1):
+        def quantise_w2(w2_codes, m0, m1):
             nc.vector.quantize_mx(
                 out=w2_codes[:, m0 * P : m1 * P].bitcast(FP8X4),
                 scales=w2_planes[:, m0 * P : m1 * P],
                 in_=w2_bf[:, m0 * P * PACK : m1 * P * PACK],
             )
 
+        last_slice = PACK - 1
         h = [sb("h%d" % t, [P, S], F32) for t in range(PACK)]
-        second = [keep.tile([P, PACK, HALF], F32, name="second0", tag="second", align_bytes=64)]
-        bent = [sb("bent%d" % e, [P, PACK, HALF], F32) for e in range(2)]
-        factor = [sb("factor%d" % e, [P, PACK, HALF], F32) for e in range(2)]
-        z = [sb("z%d" % e, [P, PACK, HALF], F32) for e in range(2)]
+        second = sb("second", [P, PACK, PAIRS], F32)
+        bent = sb("bent", [P, PACK, PAIRS], F32)
+        factor = sb("factor", [P, PACK, PAIRS], F32)
+        z = rows[:, 1:, S - PAIRS :]
         z_bf = [sb("z_bf%d" % e, [P, HALF * PACK], BF16) for e in range(2)]
         z_codes = [sb("z_codes%d" % e, [P, HALF], U32) for e in range(2)]
         z_planes = [sb("z_planes%d" % e, [P, HALF], U8) for e in range(2)]
-        cols = HALF // 16
 
         def make_h(t):
-            for u in range(S // BANK):
-                acc = psum.tile([P, BANK], F32, name="c_acc")
-                for a in range(PASSES):
-                    nc.tensor.matmul_mx(
-                        out=acc[:],
-                        lhsT=w1_codes[a][:, t * P : (t + 1) * P].bitcast(FP8X4),
-                        lhsT_scale=w1_planes[a][:, t * P : (t + 1) * P],
-                        rhs=v_words[a][:, u * BANK : (u + 1) * BANK].bitcast(FP8X4),
-                        rhs_scale=v_planes[:, a * S + u * BANK : a * S + (u + 1) * BANK],
-                        start=(a == 0),
-                        stop=(a == PASSES - 1),
-                    )
+            for (t, u), acc in product([t], "c_acc", w1_slice):
                 span = slice(u * BANK, (u + 1) * BANK)
                 nc.vector.tensor_tensor(h[t][:, span], acc[:], gates[t][:, span], MULT)
 
-        def pick_second(e, t):
-            nc.vector.tensor_copy(second[e][:, t, :], h[t][:].indirect(pos2_sb[:, e * cols : (e + 1) * cols]))
-            nc.scalar.activation(bent[e][:, t, :], second[e][:, t, :], ACT.Tanh)
-            nc.scalar.activation(factor[e][:, t, :], bent[e][:, t, :], ACT.Copy, scale=gain_sb[t][:])
+        def pick_second(t, j0, j1):
+            nc.vector.tensor_copy(second[:, t, j0:j1], h[t][:].indirect(pos2_sb[:, j0 // 16 : j1 // 16]))
+            nc.scalar.activation(bent[:, t, j0:j1], second[:, t, j0:j1], ACT.Tanh)
+            nc.scalar.activation(factor[:, t, j0:j1], bent[:, t, j0:j1], ACT.Copy, scale=gain_sb[t][:])
 
-        def pick_first(e, t):
+        def pick_first(t, j0, j1):
             nc.vector.tensor_tensor(
-                z[e][:, t, :], h[t][:].indirect(pos1_sb[:, e * cols : (e + 1) * cols]), factor[e][:, t, :], MULT
+                z[:, t, j0:j1], h[t][:].indirect(pos1_sb[:, j0 // 16 : j1 // 16]), factor[:, t, j0:j1], MULT
             )
 
         def weave(e, copy):
             copy(
                 out=z_bf[e][:].rearrange("p (c i t) -> p c t i", i=4, t=PACK),
-                in_=z[e][:].rearrange("p t (c i) -> p c t i", i=4),
+                in_=z[:, :, e * HALF : (e + 1) * HALF].rearrange("p t (c i) -> p c t i", i=4),
             )
 
         def quantise_z(e):
@@ -238,30 +250,29 @@ def tile_list_fused_passage_pairs_kernel(
                     in_=res[:].rearrange("p (s j) -> p s j", s=2),
                 )
 
-        for t in range(PACK):
-            make_gate(t)
+        make_gates([0, 1])
+        for t in range(PACK - 1):
             make_h(t)
-            pick_second(0, t)
             if t > 0:
-                pick_first(0, t - 1)
-            if t < 3:
-                cast_w2(2 * t)
-                cast_w2(2 * t + 1)
-        second.append(keep.tile([P, PACK, HALF], F32, name="second1", tag="second", align_bytes=64))
-        pick_second(1, 0)
-        pick_first(0, PACK - 1)
+                make_gates([t + 1])
+            pick_second(t, 0, PAIRS)
+            if t > 0:
+                pick_first(t - 1, 0, PAIRS)
+            cast_w2(2 * t)
+            cast_w2(2 * t + 1)
+        make_h(last_slice)
+        w2_codes = keep.tile([P, N], U32, name="w2_codes", tag="codes0", align_bytes=64)
+        quantise_w2(w2_codes, 0, 4)
+        quantise_w2(w2_codes, 4, 6)
+        pick_second(last_slice, 0, HALF)
+        pick_first(last_slice - 1, 0, HALF)
+        pick_second(last_slice, HALF, PAIRS)
+        pick_first(last_slice, 0, HALF)
         weave(0, nc.scalar.copy)
-        quantise_w2(0, 4)
-        quantise_w2(4, 6)
-        pick_second(1, 1)
-        pick_first(1, 0)
+        pick_first(last_slice - 1, HALF, PAIRS)
+        pick_first(last_slice, HALF, PAIRS)
         quantise_z(0)
-        project(0, [nc.scalar.copy] * 3)
-        pick_second(1, 2)
-        pick_first(1, 1)
-        pick_second(1, 3)
-        pick_first(1, 2)
-        pick_first(1, 3)
         weave(1, nc.vector.tensor_copy)
+        project(0, [nc.scalar.copy] * 3)
         quantise_z(1)
-        project(1, [nc.scalar.copy, nc.vector.tensor_copy, nc.scalar.copy])
+        project(1, [nc.vector.tensor_copy, nc.scalar.copy, nc.vector.tensor_copy])

@@ -14,6 +14,7 @@ U8 = mybir.dt.uint8
 FP8X4 = mybir.dt.float8_e4m3fn_x4
 FP4X4 = mybir.dt.float4_e2m1fn_x4
 MULT = mybir.AluOpType.mult
+ADD = mybir.AluOpType.add
 ACT = mybir.ActivationFunctionType
 
 P = 128
@@ -79,35 +80,24 @@ def tile_list_fused_passage_pairs_kernel(
         nc.sync.dma_start(
             out=scale_rows[0 : 16 * PASSES, :].bitcast(I32), in_=tab_scales.bitcast(I32).rearrange("a q t -> q a t")
         )
-        wg_raw = sb("wg_raw", [P, PASSES, H // 2], I32)
+        wg_raw = slot("wg_raw", [P, PASSES, H // 2], I32, 3)
         nc.sync.dma_start(out=wg_raw[:], in_=wg_words.bitcast(I32).rearrange("a p e -> p a e"))
         load_table(1)
         load_table(2)
 
         picked_rows = sb("picked_rows", [P, S], U8)
         nc.vector.tensor_copy(picked_rows[:], scale_rows[:].indirect(offs_sb[:]))
+
+        def load_w1(a, raw):
+            nc.sync.dma_start(out=raw[:], in_=w1[512 * a : 512 * (a + 1), :].rearrange("(p j) c -> p j c", j=PACK))
+
+        w1_raw = [shared.tile([P, PACK, H], F32, name="w1_raw0", offset=5120, align_bytes=64)]
+        load_w1(0, w1_raw[0])
         for q in range(4):
             (nc.sync if q % 2 else nc.scalar).dma_start(
                 out=v_planes[32 * q : 32 * q + 4, :].bitcast(I32).rearrange("r (a s) -> r a s", a=PASSES),
                 in_=picked_rows[12 * q : 12 * q + 12, :].bitcast(I32),
             )
-        v_words = [shared.tile([P, S], U32, name="v_words0", offset=1024, align_bytes=64)]
-        v_words.extend(sb("v_words%d" % a, [P, S], U32) for a in range(1, PASSES))
-        for a in range(PASSES):
-            nc.vector.tensor_copy(v_words[a][:], table[a][:].indirect(offs_sb[:]))
-
-        w1_raw = [shared.tile([P, PACK, H], F32, name="w1_raw0", offset=5120, align_bytes=64)]
-        w1_raw.extend(slot("w1_raw%d" % a, [P, PACK, H], F32, a - 1) for a in range(1, PASSES))
-        for a in range(PASSES):
-            nc.sync.dma_start(
-                out=w1_raw[a][:],
-                in_=w1[512 * a : 512 * (a + 1), :].rearrange("(p j) c -> p j c", j=PACK),
-            )
-        w2_raw = slot("w2_raw", [P, PACK, N], F32, 2)
-        w2_rows = w2.rearrange("(b t i) n -> t b i n", t=PACK, i=8)
-        for t in range(PACK):
-            nc.sync.dma_start(out=w2_raw[:, t, :], in_=w2_rows[t])
-
         wg_codes = sb("wg_codes", [P, PASSES * 2 * H], U8)
         nc.vector.tensor_copy(
             out=wg_codes[:].bitcast(I32).rearrange("p (a t b i) -> p a t b i", a=PASSES, t=PACK, i=4),
@@ -119,6 +109,20 @@ def tile_list_fused_passage_pairs_kernel(
                 out=wg_planes[live, :].bitcast(I32).rearrange("p (a t b i) -> p a t b i", a=PASSES, t=PACK, i=2),
                 in_=wg_scale_raw[live, :].bitcast(I32).rearrange("p (a b t i) -> p a t b i", a=PASSES, t=PACK, i=2),
             )
+
+        v_words = [shared.tile([P, S], U32, name="v_words0", offset=1024, align_bytes=64)]
+        v_words.extend(sb("v_words%d" % a, [P, S], U32) for a in range(1, PASSES))
+        for a in range(PASSES):
+            nc.vector.tensor_copy(v_words[a][:], table[a][:].indirect(offs_sb[:]))
+
+        w1_raw.append(slot("w1_raw1", [P, PACK, H], F32, 3))
+        load_w1(1, w1_raw[1])
+        w1_raw.append(slot("w1_raw2", [P, PACK, H], F32, 0))
+        load_w1(2, w1_raw[2])
+        w2_raw = slot("w2_raw", [P, PACK, N], F32, 1)
+        w2_rows = w2.rearrange("(b t i) n -> t b i n", t=PACK, i=8)
+        for t in range(PACK):
+            nc.sync.dma_start(out=w2_raw[:, t, :], in_=w2_rows[t])
 
         w1_bf = [sb("w1_bf%d" % a, [P, PACK * H], BF16) for a in range(PASSES)]
         w1_codes = [keep.tile([P, H], U32, name="w1_codes%d" % a, tag="codes%d" % a, align_bytes=64) for a in range(PASSES)]
@@ -145,7 +149,7 @@ def tile_list_fused_passage_pairs_kernel(
         cast_w1(last, 0, nc.vector.tensor_copy)
         for t in range(PACK):
             if t + 1 < PACK:
-                cast_w1(last, t + 1, nc.scalar.copy)
+                cast_w1(last, t + 1, nc.scalar.copy if t else nc.vector.tensor_copy)
             quantise_w1(last, t, t + 1)
 
         rows = shared.tile([P, PACK + 1, S], F32, name="rows", offset=5120, align_bytes=64)
@@ -213,7 +217,10 @@ def tile_list_fused_passage_pairs_kernel(
         def pick_second(t, j0, j1):
             nc.vector.tensor_copy(second[:, t, j0:j1], h[t][:].indirect(pos2_sb[:, j0 // 16 : j1 // 16]))
             nc.scalar.activation(bent[:, t, j0:j1], second[:, t, j0:j1], ACT.Tanh)
-            nc.scalar.activation(factor[:, t, j0:j1], bent[:, t, j0:j1], ACT.Copy, scale=gain_sb[t][:])
+            if t < last_slice:
+                nc.gpsimd.tensor_scalar(factor[:, t, j0:j1], bent[:, t, j0:j1], gain_sb[t][:], 0.0, MULT, ADD)
+            else:
+                nc.scalar.activation(factor[:, t, j0:j1], bent[:, t, j0:j1], ACT.Copy, scale=gain_sb[t][:])
 
         def pick_first(t, j0, j1):
             nc.vector.tensor_tensor(

@@ -14,14 +14,17 @@ U8 = mybir.dt.uint8
 FP8X4 = mybir.dt.float8_e4m3fn_x4
 FP4X4 = mybir.dt.float4_e2m1fn_x4
 MULT = mybir.AluOpType.mult
-ADD = mybir.AluOpType.add
 ACT = mybir.ActivationFunctionType
 
 P = 128
 PACK = 4
 PASSES = K // (P * PACK)
+LAST = PASSES - 1
 BANK = 512
+BANK_BYTES = 4 * BANK
 HALF = PAIRS // 2
+SCALE_ROWS = 16 * PASSES
+ROW0 = 48
 
 
 def tile_list_fused_passage_pairs_kernel(
@@ -31,7 +34,7 @@ def tile_list_fused_passage_pairs_kernel(
     with ExitStack() as ctx:
         keep = ctx.enter_context(tc.tile_pool(name="keep", bufs=1))
         shared = ctx.enter_context(tc.tile_pool(name="shared", bufs=1))
-        psum = ctx.enter_context(tc.psum_pool(name="psum", bufs=4))
+        psum = ctx.enter_context(tc.psum_pool(name="psum", bufs=2))
 
         def sb(name, shape, dtype):
             return keep.tile(shape, dtype, name=name, align_bytes=64)
@@ -40,35 +43,41 @@ def tile_list_fused_passage_pairs_kernel(
         pos1_sb = keep.tile([P, PAIRS // 16], U16, name="pos1_sb")
         pos2_sb = keep.tile([P, PAIRS // 16], U16, name="pos2_sb")
 
-        def slot(name, shape, dtype, n):
-            return keep.tile(shape, dtype, name=name, tag="slot%d" % n, align_bytes=64)
+        def in_turn(name, shape, dtype, tag):
+            return keep.tile(shape, dtype, name=name, tag=tag, align_bytes=64)
 
-        scale_rows = shared.tile([P, T], U8, name="scale_rows", offset=4096, align_bytes=64)
-        wg_scale_raw = sb("wg_scale_raw", [P, PASSES * H], U8)
+        def placed(name, shape, dtype, offset):
+            return shared.tile(shape, dtype, name=name, offset=offset, align_bytes=64)
+
+        scale_rows = in_turn("scale_rows", [P, T], U8, "after_scales")
+        wg_scale_raw = in_turn("wg_scale_raw", [P, PASSES * H], U8, "after_wg_scales")
         v_planes = sb("v_planes", [P, PASSES * S], U8)
-        nc.vector.memset(scale_rows[:].bitcast(I32), 0)
+        wg_planes = sb("wg_planes", [P, PASSES * H], U8)
+        nc.vector.memset(wg_planes[:].bitcast(I32), 0)
+        for q in range(4):
+            nc.scalar.dma_start(
+                out=wg_scale_raw[32 * q : 32 * q + 4, :].bitcast(I32).rearrange("r (a e) -> r a e", a=PASSES),
+                in_=wg_scales.bitcast(I32)[:, 4 * q : 4 * q + 4, :].rearrange("a r e -> r a e"),
+            )
+        nc.vector.memset(scale_rows[0:ROW0, :].bitcast(I32), 0)
+        nc.vector.memset(scale_rows[ROW0 + SCALE_ROWS :, :].bitcast(I32), 0)
         nc.vector.memset(v_planes[:].bitcast(I32), 0)
 
         warm = sb("warm", [P, 2], F32)
         nc.gpsimd.memset(warm[:, 0:1], 0.0)
         nc.scalar.activation(warm[:, 1:2], warm[:, 0:1], ACT.Sigmoid)
-        wg_planes = sb("wg_planes", [P, PASSES * H], U8)
-        nc.gpsimd.memset(wg_planes[:].bitcast(I32), 0)
 
         nc.sync.dma_start(offs_sb[:], offs)
-        nc.sync.dma_start(pos2_sb[:], pos2)
-        nc.sync.dma_start(pos1_sb[:], pos1)
+        nc.sync.dma_start(
+            out=scale_rows[ROW0 : ROW0 + SCALE_ROWS, :].bitcast(I32),
+            in_=tab_scales.bitcast(I32).rearrange("a q t -> q a t"),
+        )
         gain_sb = [sb("gain%d" % t, [P, 1], F32) for t in range(PACK)]
         gain_rows = gain.rearrange("(b t i o) -> t b i o", t=PACK, i=8, o=1)
         with nc.allow_non_contiguous_dma(reason="one gain to a partition"):
             for t in range(PACK):
                 nc.gpsimd.dma_start(out=gain_sb[t][:], in_=gain_rows[t])
-        for q in range(4):
-            nc.sync.dma_start(
-                out=wg_scale_raw[32 * q : 32 * q + 4, :].bitcast(I32).rearrange("r (a e) -> r a e", a=PASSES),
-                in_=wg_scales.bitcast(I32)[:, 4 * q : 4 * q + 4, :].rearrange("a r e -> r a e"),
-            )
-        table = [slot("table%d" % a, [P, T], U32, a) for a in range(PASSES)]
+        table = [sb("table%d" % a, [P, T], U32) for a in range(LAST)]
 
         def load_table(a):
             nc.sync.dma_start(
@@ -76,91 +85,83 @@ def tile_list_fused_passage_pairs_kernel(
                 in_=tab_words[a].rearrange("p t i -> p (t i)").bitcast(I32),
             )
 
-        load_table(0)
-        nc.sync.dma_start(
-            out=scale_rows[0 : 16 * PASSES, :].bitcast(I32), in_=tab_scales.bitcast(I32).rearrange("a q t -> q a t")
-        )
-        wg_raw = slot("wg_raw", [P, PASSES, H // 2], I32, 3)
-        nc.sync.dma_start(out=wg_raw[:], in_=wg_words.bitcast(I32).rearrange("a p e -> p a e"))
-        load_table(1)
-        load_table(2)
-
-        picked_rows = sb("picked_rows", [P, S], U8)
-        nc.vector.tensor_copy(picked_rows[:], scale_rows[:].indirect(offs_sb[:]))
-
         def load_w1(a, raw):
             nc.sync.dma_start(out=raw[:], in_=w1[512 * a : 512 * (a + 1), :].rearrange("(p j) c -> p j c", j=PACK))
 
-        w1_raw = [shared.tile([P, PACK, H], F32, name="w1_raw0", offset=5120, align_bytes=64)]
+        load_table(0)
+        nc.sync.dma_start(pos2_sb[:], pos2)
+        nc.sync.dma_start(pos1_sb[:], pos1)
+        wg_raw = placed("wg_raw", [P, PASSES, H // 2], I32, 0)
+        nc.sync.dma_start(out=wg_raw[:], in_=wg_words.bitcast(I32).rearrange("a p e -> p a e"))
+        load_table(1)
+        w1_raw = [sb("w1_raw0", [P, PACK, H], F32)]
         load_w1(0, w1_raw[0])
+
+        picked_rows = sb("picked_rows", [P, S], U8)
+        nc.vector.tensor_copy(picked_rows[:], scale_rows[:].indirect(offs_sb[:]))
         for q in range(4):
-            (nc.sync if q % 2 else nc.scalar).dma_start(
+            nc.scalar.dma_start(
                 out=v_planes[32 * q : 32 * q + 4, :].bitcast(I32).rearrange("r (a s) -> r a s", a=PASSES),
-                in_=picked_rows[12 * q : 12 * q + 12, :].bitcast(I32),
+                in_=picked_rows[ROW0 + 12 * q : ROW0 + 12 * q + 12, :].bitcast(I32),
             )
+        table.append(in_turn("table2", [P, T], U32, "after_scales"))
+        load_table(LAST)
+        v_words = [sb("v_words%d" % a, [P, S], U32) for a in range(PASSES)]
+
+        def gather_words(a):
+            nc.vector.tensor_copy(v_words[a][:], table[a][:].indirect(offs_sb[:]))
+
+        gather_words(0)
         wg_codes = sb("wg_codes", [P, PASSES * 2 * H], U8)
         nc.vector.tensor_copy(
             out=wg_codes[:].bitcast(I32).rearrange("p (a t b i) -> p a t b i", a=PASSES, t=PACK, i=4),
             in_=wg_raw[:].rearrange("p a (b t i) -> p a t b i", t=PACK, i=4),
         )
+        w1_raw.append(placed("w1_raw1", [P, PACK, H], F32, 0))
+        load_w1(1, w1_raw[1])
         for q in range(4):
             live = slice(32 * q, 32 * q + 4)
             nc.vector.tensor_copy(
                 out=wg_planes[live, :].bitcast(I32).rearrange("p (a t b i) -> p a t b i", a=PASSES, t=PACK, i=2),
                 in_=wg_scale_raw[live, :].bitcast(I32).rearrange("p (a b t i) -> p a t b i", a=PASSES, t=PACK, i=2),
             )
-
-        v_words = [shared.tile([P, S], U32, name="v_words0", offset=1024, align_bytes=64)]
-        v_words.extend(sb("v_words%d" % a, [P, S], U32) for a in range(1, PASSES))
-        for a in range(PASSES):
-            nc.vector.tensor_copy(v_words[a][:], table[a][:].indirect(offs_sb[:]))
-
-        w1_raw.append(slot("w1_raw1", [P, PACK, H], F32, 3))
-        load_w1(1, w1_raw[1])
-        w1_raw.append(slot("w1_raw2", [P, PACK, H], F32, 0))
-        load_w1(2, w1_raw[2])
-        w2_raw = slot("w2_raw", [P, PACK, N], F32, 1)
+        w1_raw.append(in_turn("w1_raw2", [P, PACK, H], F32, "after_wg_scales"))
+        load_w1(LAST, w1_raw[LAST])
+        gather_words(1)
+        gather_words(LAST)
+        w2_raw = in_turn("w2_raw", [P, PACK, N], F32, "after_scales")
         w2_rows = w2.rearrange("(b t i) n -> t b i n", t=PACK, i=8)
         for t in range(PACK):
             nc.sync.dma_start(out=w2_raw[:, t, :], in_=w2_rows[t])
 
         w1_bf = [sb("w1_bf%d" % a, [P, PACK * H], BF16) for a in range(PASSES)]
-        w1_codes = [keep.tile([P, H], U32, name="w1_codes%d" % a, tag="codes%d" % a, align_bytes=64) for a in range(PASSES)]
+        w1_codes = [sb("w1_codes%d" % a, [P, H], U32) for a in range(LAST)]
+        last_codes = []
         w1_planes = [sb("w1_planes%d" % a, [P, H], U8) for a in range(PASSES)]
 
-        def cast_w1(a, t, copy):
+        def round_w1(a, t, copy):
             copy(
-                out=w1_bf[a][:, t * H : (t + 1) * H].rearrange("p (b h i j) -> p b h j i", h=2, i=4, j=PACK),
-                in_=w1_raw[a][:].rearrange("p j (b t h i) -> p t b h j i", t=PACK, h=2, i=4)[:, t],
+                out=w1_bf[a][:, t * H : (t + 1) * H].rearrange("p (b f i j) -> p b f j i", f=2, i=4, j=PACK),
+                in_=w1_raw[a][:].rearrange("p j (b t f i) -> p t b f j i", t=PACK, f=2, i=4)[:, t],
             )
 
-        def quantise_w1(a, t0, t1):
+        def quantise_w1(a):
+            nc.vector.quantize_mx(out=w1_codes[a][:].bitcast(FP8X4), scales=w1_planes[a][:], in_=w1_bf[a][:])
+
+        def quantise_last(t):
+            name = "last_codes%d" % t
+            last_codes.append(placed(name, [P, P], U32, BANK_BYTES * (t - 1)) if t else sb(name, [P, P], U32))
             nc.vector.quantize_mx(
-                out=w1_codes[a][:, t0 * P : t1 * P].bitcast(FP8X4),
-                scales=w1_planes[a][:, t0 * P : t1 * P],
-                in_=w1_bf[a][:, t0 * H : t1 * H],
+                out=last_codes[t][:].bitcast(FP8X4),
+                scales=w1_planes[LAST][:, t * P : (t + 1) * P],
+                in_=w1_bf[LAST][:, t * H : (t + 1) * H],
             )
 
-        for a in range(PASSES - 1):
-            for t in range(PACK):
-                cast_w1(a, t, nc.scalar.copy if a == 0 else nc.vector.tensor_copy)
-            quantise_w1(a, 0, PACK)
-        last = PASSES - 1
-        cast_w1(last, 0, nc.vector.tensor_copy)
-        for t in range(PACK):
-            if t + 1 < PACK:
-                cast_w1(last, t + 1, nc.scalar.copy if t else nc.vector.tensor_copy)
-            quantise_w1(last, t, t + 1)
-
-        rows = shared.tile([P, PACK + 1, S], F32, name="rows", offset=5120, align_bytes=64)
-        gates = [rows[:, t, :] for t in range(PACK)]
-
-        def product(slices, tag, stationary):
-            groups = [(t, u) for t in slices for u in range(S // BANK)]
-            accs = [psum.tile([P, BANK], F32, name=tag) for group in groups]
+        def product(t, banks, stationary):
+            accs = [psum.tile([P, BANK], F32, name=banks) for u in range(S // BANK)]
             for a in range(PASSES):
-                for (t, u), acc in zip(groups, accs):
-                    codes, planes = stationary(a, t)
+                codes, planes = stationary(a, t)
+                for u, acc in enumerate(accs):
                     nc.tensor.matmul_mx(
                         out=acc[:],
                         lhsT=codes,
@@ -168,77 +169,71 @@ def tile_list_fused_passage_pairs_kernel(
                         rhs=v_words[a][:, u * BANK : (u + 1) * BANK].bitcast(FP8X4),
                         rhs_scale=v_planes[:, a * S + u * BANK : a * S + (u + 1) * BANK],
                         start=(a == 0),
-                        stop=(a == PASSES - 1),
+                        stop=(a == LAST),
                     )
-            return zip(groups, accs)
+            return accs
 
         def wg_slice(a, t):
             col = a * H + t * P
             return wg_codes[:, 2 * col : 2 * (col + P)].bitcast(FP4X4), wg_planes[:, col : col + P]
 
         def w1_slice(a, t):
-            return w1_codes[a][:, t * P : (t + 1) * P].bitcast(FP8X4), w1_planes[a][:, t * P : (t + 1) * P]
+            codes = w1_codes[a][:, t * P : (t + 1) * P] if a < LAST else last_codes[t][:]
+            return codes.bitcast(FP8X4), w1_planes[a][:, t * P : (t + 1) * P]
 
-        def make_gates(slices):
-            for (t, u), acc in product(slices, "g_acc", wg_slice):
-                nc.scalar.activation(gates[t][:, u * BANK : (u + 1) * BANK], acc[:], ACT.Sigmoid)
+        def sigmoids(t, accs):
+            for u, acc in enumerate(accs):
+                nc.scalar.activation(gates[t][u], acc[:], ACT.Sigmoid)
 
         w2_bf = sb("w2_bf", [P, N * PACK], BF16)
         w2_planes = sb("w2_planes", [P, N], U8)
+        w2_codes = sb("w2_codes", [P, N], U32)
 
-        def cast_w2(m):
+        def round_w2(m):
             nc.scalar.copy(
                 out=w2_bf[:, m * P * PACK : (m + 1) * P * PACK].rearrange("p (c i t) -> p c t i", i=4, t=PACK),
                 in_=w2_raw[:, :, m * P : (m + 1) * P].rearrange("p t (c i) -> p c t i", i=4),
             )
 
-        def quantise_w2(w2_codes, m0, m1):
+        def quantise_w2(m0, m1):
             nc.vector.quantize_mx(
                 out=w2_codes[:, m0 * P : m1 * P].bitcast(FP8X4),
                 scales=w2_planes[:, m0 * P : m1 * P],
                 in_=w2_bf[:, m0 * P * PACK : m1 * P * PACK],
             )
 
-        last_slice = PACK - 1
         h = [sb("h%d" % t, [P, S], F32) for t in range(PACK)]
         second = sb("second", [P, PACK, PAIRS], F32)
         bent = sb("bent", [P, PACK, PAIRS], F32)
         factor = sb("factor", [P, PACK, PAIRS], F32)
-        z = rows[:, 1:, S - PAIRS :]
-        z_bf = [sb("z_bf%d" % e, [P, HALF * PACK], BF16) for e in range(2)]
+        z_bf_back = sb("z_bf_back", [P, HALF * PACK], BF16)
         z_codes = [sb("z_codes%d" % e, [P, HALF], U32) for e in range(2)]
         z_planes = [sb("z_planes%d" % e, [P, HALF], U8) for e in range(2)]
 
-        def make_h(t):
-            for (t, u), acc in product([t], "c_acc", w1_slice):
-                span = slice(u * BANK, (u + 1) * BANK)
-                nc.vector.tensor_tensor(h[t][:, span], acc[:], gates[t][:, span], MULT)
+        def make_h(t, banks):
+            for u, acc in enumerate(product(t, banks, w1_slice)):
+                nc.vector.tensor_tensor(h[t][:, u * BANK : (u + 1) * BANK], acc[:], gates[t][u], MULT)
 
-        def pick_second(t, j0, j1):
+        def pick_second(t, j0, j1, dest):
             nc.vector.tensor_copy(second[:, t, j0:j1], h[t][:].indirect(pos2_sb[:, j0 // 16 : j1 // 16]))
             nc.scalar.activation(bent[:, t, j0:j1], second[:, t, j0:j1], ACT.Tanh)
-            if t < last_slice:
-                nc.gpsimd.tensor_scalar(factor[:, t, j0:j1], bent[:, t, j0:j1], gain_sb[t][:], 0.0, MULT, ADD)
-            else:
-                nc.scalar.activation(factor[:, t, j0:j1], bent[:, t, j0:j1], ACT.Copy, scale=gain_sb[t][:])
+            nc.scalar.activation(dest, bent[:, t, j0:j1], ACT.Copy, scale=gain_sb[t][:])
 
-        def pick_first(t, j0, j1):
-            nc.vector.tensor_tensor(
-                z[:, t, j0:j1], h[t][:].indirect(pos1_sb[:, j0 // 16 : j1 // 16]), factor[:, t, j0:j1], MULT
-            )
+        def pick_first(t, j0, j1, other, dest):
+            nc.vector.tensor_tensor(dest, h[t][:].indirect(pos1_sb[:, j0 // 16 : j1 // 16]), other, MULT)
 
-        def weave(e, copy):
+        def weave(z, z_bf, copy):
             copy(
-                out=z_bf[e][:].rearrange("p (c i t) -> p c t i", i=4, t=PACK),
-                in_=z[:, :, e * HALF : (e + 1) * HALF].rearrange("p t (c i) -> p c t i", i=4),
+                out=z_bf.rearrange("p (c i t) -> p c t i", i=4, t=PACK),
+                in_=z.rearrange("p t (c i) -> p c t i", i=4),
             )
 
-        def quantise_z(e):
-            nc.vector.quantize_mx(out=z_codes[e][:].bitcast(FP8X4), scales=z_planes[e][:], in_=z_bf[e][:])
+        def quantise_z(e, z_bf):
+            nc.vector.quantize_mx(out=z_codes[e][:].bitcast(FP8X4), scales=z_planes[e][:], in_=z_bf)
 
         def project(e, copies):
-            for g in range(N // (2 * P)):
-                acc = psum.tile([P, BANK], F32, name="g_acc")
+            for g, copy in enumerate(copies):
+                acc = psum.tile([P, BANK], F32, name=("acc_a", "acc_b")[g % 2])
                 for s in range(2):
                     m = 2 * g + s
                     nc.tensor.matmul_mx(
@@ -251,35 +246,59 @@ def tile_list_fused_passage_pairs_kernel(
                         stop=True,
                     )
                 res = sb("res%d_%d" % (e, g), [P, BANK], F32)
-                copies[g](out=res[:], in_=acc[:])
+                copy(out=res[:], in_=acc[:])
                 nc.sync.dma_start(
                     out=out[2 * g * P : 2 * (g + 1) * P, e * HALF : (e + 1) * HALF].rearrange("(s p) j -> p s j", p=P),
                     in_=res[:].rearrange("p (s j) -> p s j", s=2),
                 )
 
-        make_gates([0, 1])
-        for t in range(PACK - 1):
-            make_h(t)
-            if t > 0:
-                make_gates([t + 1])
-            pick_second(t, 0, PAIRS)
-            if t > 0:
-                pick_first(t - 1, 0, PAIRS)
-            cast_w2(2 * t)
-            cast_w2(2 * t + 1)
-        make_h(last_slice)
-        w2_codes = keep.tile([P, N], U32, name="w2_codes", tag="codes0", align_bytes=64)
-        quantise_w2(w2_codes, 0, 4)
-        quantise_w2(w2_codes, 4, 6)
-        pick_second(last_slice, 0, HALF)
-        pick_first(last_slice - 1, 0, HALF)
-        pick_second(last_slice, HALF, PAIRS)
-        pick_first(last_slice, 0, HALF)
-        weave(0, nc.scalar.copy)
-        pick_first(last_slice - 1, HALF, PAIRS)
-        pick_first(last_slice, HALF, PAIRS)
-        quantise_z(0)
-        weave(1, nc.vector.tensor_copy)
-        project(0, [nc.scalar.copy] * 3)
-        quantise_z(1)
-        project(1, [nc.vector.tensor_copy, nc.scalar.copy, nc.vector.tensor_copy])
+        on_scalar, on_vector = nc.scalar.copy, nc.vector.tensor_copy
+        for a in range(LAST):
+            for t in range(PACK):
+                round_w1(a, t, on_vector if a == 1 and t < 2 else on_scalar)
+            quantise_w1(a)
+
+        first_gate = product(0, "acc_a", wg_slice)
+        backs = placed("backs", [P, PACK + 1, BANK], F32, 3 * BANK_BYTES)
+        fronts = [placed("front%d" % t, [P, BANK], F32, BANK_BYTES * t) for t in range(PACK - 1)]
+        fronts.append(sb("front3", [P, BANK], F32))
+        gates = [(fronts[t][:], backs[:, t, :]) for t in range(PACK)]
+        z_front = backs[:, 1:, BANK - HALF :]
+        last_factor = in_turn("last_factor", [P, HALF], F32, "after_front")
+
+        round_w1(LAST, 0, on_vector)
+        sigmoids(0, first_gate)
+        quantise_last(0)
+        round_w1(LAST, 1, on_scalar)
+        make_h(0, "acc_x")
+        for t in range(1, PACK):
+            sigmoids(t, product(t, "acc_b" if t == 1 else "acc_x", wg_slice))
+            quantise_last(t)
+            if t + 1 < PACK:
+                round_w1(LAST, t + 1, on_scalar)
+            pick_second(t - 1, 0, PAIRS, factor[:, t - 1, :])
+            if t > 1:
+                pick_first(t - 2, 0, HALF, factor[:, t - 2, 0:HALF], z_front[:, t - 2, :])
+            if t + 1 == PACK:
+                for m in range(N // P):
+                    round_w2(m)
+            make_h(t, "acc_y")
+
+        end = PACK - 1
+        pick_second(end, 0, HALF, last_factor[:])
+        pick_first(end - 1, 0, HALF, factor[:, end - 1, 0:HALF], z_front[:, end - 1, :])
+        pick_second(end, HALF, PAIRS, factor[:, end, HALF:PAIRS])
+        quantise_w2(0, 4)
+        pick_first(end, 0, HALF, last_factor[:], z_front[:, end, :])
+        z_back = in_turn("z_back", [P, PACK * HALF], F32, "after_front")
+        z_bf_front = z_back[:, 2 * HALF :].bitcast(BF16)
+        weave(z_front, z_bf_front, on_scalar)
+        quantise_w2(4, 6)
+        for t in range(PACK):
+            pick_first(t, HALF, PAIRS, factor[:, t, HALF:PAIRS], z_back[:, HALF * t : HALF * (t + 1)])
+            if t == 1:
+                quantise_z(0, z_bf_front)
+                project(0, [on_scalar] * 3)
+        weave(z_back[:].rearrange("p (t j) -> p t j", t=PACK), z_bf_back[:], on_vector)
+        quantise_z(1, z_bf_back[:])
+        project(1, [on_vector, on_scalar, on_vector])

@@ -21,9 +21,10 @@ PACK = 4
 PASSES = K // (P * PACK)
 LAST = PASSES - 1
 BANK = 512
-BANK_BYTES = 4 * BANK
 HALF = PAIRS // 2
+SIDE = H // 2
 SCALE_ROWS = 16 * PASSES
+PLANE = S + H
 ROW0 = 48
 
 
@@ -39,45 +40,39 @@ def tile_list_fused_passage_pairs_kernel(
         def sb(name, shape, dtype):
             return keep.tile(shape, dtype, name=name, align_bytes=64)
 
-        offs_sb = keep.tile([P, S // 16], U16, name="offs_sb")
-        pos1_sb = keep.tile([P, PAIRS // 16], U16, name="pos1_sb")
-        pos2_sb = keep.tile([P, PAIRS // 16], U16, name="pos2_sb")
-
         def in_turn(name, shape, dtype, tag):
             return keep.tile(shape, dtype, name=name, tag=tag, align_bytes=64)
 
         def placed(name, shape, dtype, offset):
             return shared.tile(shape, dtype, name=name, offset=offset, align_bytes=64)
 
-        scale_rows = in_turn("scale_rows", [P, T], U8, "after_scales")
-        wg_scale_raw = in_turn("wg_scale_raw", [P, PASSES * H], U8, "after_wg_scales")
-        v_planes = sb("v_planes", [P, PASSES * S], U8)
-        wg_planes = sb("wg_planes", [P, PASSES * H], U8)
-        nc.vector.memset(wg_planes[:].bitcast(I32), 0)
-        for q in range(4):
-            nc.scalar.dma_start(
-                out=wg_scale_raw[32 * q : 32 * q + 4, :].bitcast(I32).rearrange("r (a e) -> r a e", a=PASSES),
-                in_=wg_scales.bitcast(I32)[:, 4 * q : 4 * q + 4, :].rearrange("a r e -> r a e"),
-            )
-        nc.vector.memset(scale_rows[0:ROW0, :].bitcast(I32), 0)
-        nc.vector.memset(scale_rows[ROW0 + SCALE_ROWS :, :].bitcast(I32), 0)
-        nc.vector.memset(v_planes[:].bitcast(I32), 0)
+        offs_sb = keep.tile([P, S // 16], U16, name="offs_sb")
+        pos1_sb = keep.tile([P, PAIRS // 16], U16, name="pos1_sb")
+        pos2_sb = keep.tile([P, PAIRS // 16], U16, name="pos2_sb")
 
-        warm = sb("warm", [P, 2], F32)
-        nc.gpsimd.memset(warm[:, 0:1], 0.0)
-        nc.scalar.activation(warm[:, 1:2], warm[:, 0:1], ACT.Sigmoid)
+        scale_rows = sb("scale_rows", [P, T], U8)
+        wg_scale_rows = sb("wg_scale_rows", [P, H], U8)
+        planes = sb("planes", [P, PASSES * PLANE], U8)
+
+        def load_scales(rows, scales, queue):
+            for a in range(PASSES):
+                queue.dma_start(
+                    out=rows[ROW0 + a : ROW0 + SCALE_ROWS : PASSES, :].bitcast(I32), in_=scales.bitcast(I32)[a]
+                )
 
         nc.sync.dma_start(offs_sb[:], offs)
-        nc.sync.dma_start(
-            out=scale_rows[ROW0 : ROW0 + SCALE_ROWS, :].bitcast(I32),
-            in_=tab_scales.bitcast(I32).rearrange("a q t -> q a t"),
-        )
-        gain_sb = [sb("gain%d" % t, [P, 1], F32) for t in range(PACK)]
-        gain_rows = gain.rearrange("(b t i o) -> t b i o", t=PACK, i=8, o=1)
-        with nc.allow_non_contiguous_dma(reason="one gain to a partition"):
-            for t in range(PACK):
-                nc.gpsimd.dma_start(out=gain_sb[t][:], in_=gain_rows[t])
-        table = [sb("table%d" % a, [P, T], U32) for a in range(LAST)]
+        load_scales(scale_rows, tab_scales, nc.sync)
+        load_scales(wg_scale_rows, wg_scales, nc.scalar)
+        for rows in (scale_rows, wg_scale_rows):
+            nc.vector.memset(rows[0:ROW0, :].bitcast(I32), 0)
+            nc.vector.memset(rows[ROW0 + SCALE_ROWS :, :].bitcast(I32), 0)
+        nc.vector.memset(planes[:].bitcast(I32), 0)
+
+        warm = sb("warm", [P, 2], F32)
+        nc.vector.memset(warm[:, 0:1], 0.0)
+        nc.scalar.activation(warm[:, 1:2], warm[:, 0:1], ACT.Sigmoid)
+
+        table = [placed("table%d" % a, [P, T], U32, 4 * T * a) for a in range(PASSES)]
 
         def load_table(a):
             nc.sync.dma_start(
@@ -85,89 +80,103 @@ def tile_list_fused_passage_pairs_kernel(
                 in_=tab_words[a].rearrange("p t i -> p (t i)").bitcast(I32),
             )
 
-        def load_w1(a, raw):
-            nc.sync.dma_start(out=raw[:], in_=w1[512 * a : 512 * (a + 1), :].rearrange("(p j) c -> p j c", j=PACK))
+        w1_raw = {}
+
+        def load_w1(side, a, place, where):
+            w1_raw[side, a] = place("w1_raw%d_%d" % (side, a), [P, PACK, SIDE], F32, where)
+            rows = w1[512 * a : 512 * (a + 1), side * SIDE : (side + 1) * SIDE]
+            nc.sync.dma_start(out=w1_raw[side, a][:], in_=rows.rearrange("(p j) c -> p j c", j=PACK))
 
         load_table(0)
         nc.sync.dma_start(pos2_sb[:], pos2)
         nc.sync.dma_start(pos1_sb[:], pos1)
-        wg_raw = placed("wg_raw", [P, PASSES, H // 2], I32, 0)
+        wg_raw = in_turn("wg_raw", [P, PASSES, H // 2], I32, "after_wg")
         nc.sync.dma_start(out=wg_raw[:], in_=wg_words.bitcast(I32).rearrange("a p e -> p a e"))
         load_table(1)
-        w1_raw = [sb("w1_raw0", [P, PACK, H], F32)]
-        load_w1(0, w1_raw[0])
+        load_table(LAST)
 
         picked_rows = sb("picked_rows", [P, S], U8)
         nc.vector.tensor_copy(picked_rows[:], scale_rows[:].indirect(offs_sb[:]))
+        both_rows = in_turn("both_rows", [P, PLANE], U8, "after_moves")
+        nc.vector.tensor_copy(both_rows[:, 0:S].bitcast(I32), picked_rows[:].bitcast(I32))
+        by_block = wg_scale_rows[:].bitcast(I32).rearrange("p (b g w) -> p g b w", g=2, w=2)
+        nc.vector.tensor_copy(
+            out=both_rows[:, S : S + SIDE].bitcast(I32).rearrange("p (b w) -> p b w", w=2), in_=by_block[:, 0]
+        )
+        nc.vector.tensor_copy(
+            out=both_rows[:, S + SIDE :].bitcast(I32).rearrange("p (t b) -> p t b", t=2),
+            in_=by_block[:, 1].rearrange("p b t -> p t b"),
+        )
         for q in range(4):
-            nc.scalar.dma_start(
-                out=v_planes[32 * q : 32 * q + 4, :].bitcast(I32).rearrange("r (a s) -> r a s", a=PASSES),
-                in_=picked_rows[ROW0 + 12 * q : ROW0 + 12 * q + 12, :].bitcast(I32),
+            (nc.scalar if q % 2 else nc.sync).dma_start(
+                out=planes[32 * q : 32 * q + 4, :].bitcast(I32).rearrange("r (a s) -> r a s", a=PASSES),
+                in_=both_rows[ROW0 + 12 * q : ROW0 + 12 * q + 12, :].bitcast(I32),
             )
-        table.append(in_turn("table2", [P, T], U32, "after_scales"))
-        load_table(LAST)
         v_words = [sb("v_words%d" % a, [P, S], U32) for a in range(PASSES)]
 
-        def gather_words(a):
-            nc.vector.tensor_copy(v_words[a][:], table[a][:].indirect(offs_sb[:]))
+        def gather_words(a, s0, s1):
+            nc.vector.tensor_copy(v_words[a][:, s0:s1], table[a][:].indirect(offs_sb[:, s0 // 16 : s1 // 16]))
 
-        gather_words(0)
+        gather_words(0, 0, S)
+        for a in range(LAST):
+            load_w1(0, a, placed, 2 * T * a)
         wg_codes = sb("wg_codes", [P, PASSES * 2 * H], U8)
+        dealt = wg_codes[:].bitcast(I32).rearrange("p (a g c) -> p g a c", a=PASSES, g=2)
+        by_block = wg_raw[:].rearrange("p a (b g w) -> p g a b w", g=2, w=4)
+        nc.vector.tensor_copy(out=dealt[:, 0].rearrange("p a (b w) -> p a b w", w=4), in_=by_block[:, 0])
         nc.vector.tensor_copy(
-            out=wg_codes[:].bitcast(I32).rearrange("p (a t b i) -> p a t b i", a=PASSES, t=PACK, i=4),
-            in_=wg_raw[:].rearrange("p a (b t i) -> p a t b i", t=PACK, i=4),
+            out=dealt[:, 1].rearrange("p a (t b w) -> p a t b w", t=2, w=2),
+            in_=by_block[:, 1].rearrange("p a b (t w) -> p a t b w", t=2),
         )
-        w1_raw.append(placed("w1_raw1", [P, PACK, H], F32, 0))
-        load_w1(1, w1_raw[1])
-        for q in range(4):
-            live = slice(32 * q, 32 * q + 4)
-            nc.vector.tensor_copy(
-                out=wg_planes[live, :].bitcast(I32).rearrange("p (a t b i) -> p a t b i", a=PASSES, t=PACK, i=2),
-                in_=wg_scale_raw[live, :].bitcast(I32).rearrange("p (a b t i) -> p a t b i", a=PASSES, t=PACK, i=2),
-            )
-        w1_raw.append(in_turn("w1_raw2", [P, PACK, H], F32, "after_wg_scales"))
-        load_w1(LAST, w1_raw[LAST])
-        gather_words(1)
-        gather_words(LAST)
-        w2_raw = in_turn("w2_raw", [P, PACK, N], F32, "after_scales")
-        w2_rows = w2.rearrange("(b t i) n -> t b i n", t=PACK, i=8)
-        for t in range(PACK):
-            nc.sync.dma_start(out=w2_raw[:, t, :], in_=w2_rows[t])
+        load_w1(0, LAST, in_turn, "after_wg")
+        load_w1(1, 0, in_turn, "after_moves")
+        gather_words(1, 0, S)
+        for a in range(1, PASSES):
+            load_w1(1, a, placed, 2 * T * (a + 1))
 
-        w1_bf = [sb("w1_bf%d" % a, [P, PACK * H], BF16) for a in range(PASSES)]
-        w1_codes = [sb("w1_codes%d" % a, [P, H], U32) for a in range(LAST)]
-        last_codes = []
-        w1_planes = [sb("w1_planes%d" % a, [P, H], U8) for a in range(PASSES)]
+        low_bf, high_bf = {}, {}
+        low_codes = [sb("low_codes%d" % t, [P, PASSES * P], U32) for t in range(2)]
+        low_planes = [sb("low_planes%d" % t, [P, PASSES * P], U8) for t in range(2)]
+        high_codes = [sb("high_codes%d" % a, [P, 2 * P], U32) for a in range(PASSES)]
+        high_planes = [sb("high_planes%d" % a, [P, 2 * P], U8) for a in range(PASSES)]
 
-        def round_w1(a, t, copy):
+        def round_low(side, a, copy):
+            low_bf[side, a] = in_turn("low_bf%d_%d" % (side, a), [P, H], BF16, "low_bf%d_%d" % (side, a))
             copy(
-                out=w1_bf[a][:, t * H : (t + 1) * H].rearrange("p (b f i j) -> p b f j i", f=2, i=4, j=PACK),
-                in_=w1_raw[a][:].rearrange("p j (b t f i) -> p t b f j i", t=PACK, f=2, i=4)[:, t],
+                out=low_bf[side, a][:].rearrange("p (b f i j) -> p b f j i", f=2, i=4, j=PACK),
+                in_=w1_raw[side, a][:].rearrange("p j (b g f i) -> p g b f j i", g=2, f=2, i=4)[:, 0],
             )
 
-        def quantise_w1(a):
-            nc.vector.quantize_mx(out=w1_codes[a][:].bitcast(FP8X4), scales=w1_planes[a][:], in_=w1_bf[a][:])
+        def round_high(side, a, copy):
+            if side == 0:
+                tag = "low_bf0_%d" % a if a == LAST else "high_bf%d" % a
+                high_bf[a] = in_turn("high_bf%d" % a, [P, 2 * H], BF16, tag)
+            copy(
+                out=high_bf[a][:].rearrange("p (t s b i j) -> p s t b j i", t=2, s=2, i=4, j=PACK)[:, side],
+                in_=w1_raw[side, a][:].rearrange("p j (b g t i) -> p g t b j i", g=2, t=2, i=4)[:, 1],
+            )
 
-        def quantise_last(t):
-            name = "last_codes%d" % t
-            last_codes.append(placed(name, [P, P], U32, BANK_BYTES * (t - 1)) if t else sb(name, [P, P], U32))
+        def quantise_low(t, a):
             nc.vector.quantize_mx(
-                out=last_codes[t][:].bitcast(FP8X4),
-                scales=w1_planes[LAST][:, t * P : (t + 1) * P],
-                in_=w1_bf[LAST][:, t * H : (t + 1) * H],
+                out=low_codes[t][:, a * P : (a + 1) * P].bitcast(FP8X4),
+                scales=low_planes[t][:, a * P : (a + 1) * P],
+                in_=low_bf[t, a][:],
             )
+
+        def quantise_high(a):
+            nc.vector.quantize_mx(out=high_codes[a][:].bitcast(FP8X4), scales=high_planes[a][:], in_=high_bf[a][:])
 
         def product(t, banks, stationary):
             accs = [psum.tile([P, BANK], F32, name=banks) for u in range(S // BANK)]
             for a in range(PASSES):
-                codes, planes = stationary(a, t)
+                codes, scales = stationary(a, t)
                 for u, acc in enumerate(accs):
                     nc.tensor.matmul_mx(
                         out=acc[:],
                         lhsT=codes,
-                        lhsT_scale=planes,
+                        lhsT_scale=scales,
                         rhs=v_words[a][:, u * BANK : (u + 1) * BANK].bitcast(FP8X4),
-                        rhs_scale=v_planes[:, a * S + u * BANK : a * S + (u + 1) * BANK],
+                        rhs_scale=planes[:, a * PLANE + u * BANK : a * PLANE + (u + 1) * BANK],
                         start=(a == 0),
                         stop=(a == LAST),
                     )
@@ -175,19 +184,25 @@ def tile_list_fused_passage_pairs_kernel(
 
         def wg_slice(a, t):
             col = a * H + t * P
-            return wg_codes[:, 2 * col : 2 * (col + P)].bitcast(FP4X4), wg_planes[:, col : col + P]
+            first = a * PLANE + S + t * P
+            return wg_codes[:, 2 * col : 2 * (col + P)].bitcast(FP4X4), planes[:, first : first + P]
 
         def w1_slice(a, t):
-            codes = w1_codes[a][:, t * P : (t + 1) * P] if a < LAST else last_codes[t][:]
-            return codes.bitcast(FP8X4), w1_planes[a][:, t * P : (t + 1) * P]
+            if t < 2:
+                return low_codes[t][:, a * P : (a + 1) * P].bitcast(FP8X4), low_planes[t][:, a * P : (a + 1) * P]
+            cols = slice((t - 2) * P, (t - 1) * P)
+            return high_codes[a][:, cols].bitcast(FP8X4), high_planes[a][:, cols]
+
+        gates = {}
 
         def sigmoids(t, accs):
             for u, acc in enumerate(accs):
-                nc.scalar.activation(gates[t][u], acc[:], ACT.Sigmoid)
+                name = "gate%d_%d" % (t, u)
+                gates[t, u] = sb(name, [P, BANK], F32) if t else placed(name, [P, BANK], F32, 2 * T * u)
+                nc.scalar.activation(gates[t, u][:], acc[:], ACT.Sigmoid)
 
         w2_bf = sb("w2_bf", [P, N * PACK], BF16)
         w2_planes = sb("w2_planes", [P, N], U8)
-        w2_codes = sb("w2_codes", [P, N], U32)
 
         def round_w2(m):
             nc.scalar.copy(
@@ -203,102 +218,150 @@ def tile_list_fused_passage_pairs_kernel(
             )
 
         h = [sb("h%d" % t, [P, S], F32) for t in range(PACK)]
-        second = sb("second", [P, PACK, PAIRS], F32)
         bent = sb("bent", [P, PACK, PAIRS], F32)
-        factor = sb("factor", [P, PACK, PAIRS], F32)
-        z_bf_back = sb("z_bf_back", [P, HALF * PACK], BF16)
-        z_codes = [sb("z_codes%d" % e, [P, HALF], U32) for e in range(2)]
-        z_planes = [sb("z_planes%d" % e, [P, HALF], U8) for e in range(2)]
+        z = [sb("z%d" % e, [P, PACK * HALF], F32) for e in range(2)]
+        z_codes = sb("z_codes", [P, PAIRS], U32)
+        z_planes = sb("z_planes", [P, PAIRS], U8)
 
-        def make_h(t, banks):
-            for u, acc in enumerate(product(t, banks, w1_slice)):
-                nc.vector.tensor_tensor(h[t][:, u * BANK : (u + 1) * BANK], acc[:], gates[t][u], MULT)
+        def make_h(t, accs):
+            for u, acc in enumerate(accs):
+                cols = slice(u * BANK, (u + 1) * BANK)
+                nc.vector.tensor_tensor(h[t][:, cols], acc[:], gates[t, u][:], MULT)
 
         def pick_second(t, j0, j1, dest):
-            nc.vector.tensor_copy(second[:, t, j0:j1], h[t][:].indirect(pos2_sb[:, j0 // 16 : j1 // 16]))
-            nc.scalar.activation(bent[:, t, j0:j1], second[:, t, j0:j1], ACT.Tanh)
+            nc.vector.tensor_copy(dest, h[t][:].indirect(pos2_sb[:, j0 // 16 : j1 // 16]))
+
+        def bend(t, j0, j1, second, dest):
+            nc.scalar.activation(bent[:, t, j0:j1], second, ACT.Tanh)
             nc.scalar.activation(dest, bent[:, t, j0:j1], ACT.Copy, scale=gain_sb[t][:])
 
         def pick_first(t, j0, j1, other, dest):
             nc.vector.tensor_tensor(dest, h[t][:].indirect(pos1_sb[:, j0 // 16 : j1 // 16]), other, MULT)
 
-        def weave(z, z_bf, copy):
+        def move_low(t, z_low):
+            for e in range(2):
+                nc.sync.dma_start(
+                    out=z[e][64 * t : 64 * (t + 1), 0 : 2 * HALF].rearrange("p (s j) -> p s j", s=2),
+                    in_=z_low[:, e * HALF : (e + 1) * HALF],
+                )
+
+        def weave(j0, j1, z_bf, copy):
+            e = j0 // HALF
             copy(
                 out=z_bf.rearrange("p (c i t) -> p c t i", i=4, t=PACK),
-                in_=z.rearrange("p t (c i) -> p c t i", i=4),
+                in_=z[e][:].rearrange("p (t c i) -> p c t i", t=PACK, i=4)[:, (j0 - e * HALF) // 4 : (j1 - e * HALF) // 4],
             )
 
-        def quantise_z(e, z_bf):
-            nc.vector.quantize_mx(out=z_codes[e][:].bitcast(FP8X4), scales=z_planes[e][:], in_=z_bf)
+        def quantise_z(j0, j1, z_bf):
+            nc.vector.quantize_mx(out=z_codes[:, j0:j1].bitcast(FP8X4), scales=z_planes[:, j0:j1], in_=z_bf)
 
-        def project(e, copies):
+        def project(j0, j1, banks, copies):
+            width = j1 - j0
+            blocks = N // P // len(banks)
             for g, copy in enumerate(copies):
-                acc = psum.tile([P, BANK], F32, name=("acc_a", "acc_b")[g % 2])
-                for s in range(2):
-                    m = 2 * g + s
+                acc = psum.tile([P, BANK], F32, name=banks[g])
+                for s in range(blocks):
+                    m = blocks * g + s
                     nc.tensor.matmul_mx(
-                        out=acc[:, s * HALF : (s + 1) * HALF],
+                        out=acc[:, s * width : (s + 1) * width],
                         lhsT=w2_codes[:, m * P : (m + 1) * P].bitcast(FP8X4),
                         lhsT_scale=w2_planes[:, m * P : (m + 1) * P],
-                        rhs=z_codes[e][:].bitcast(FP8X4),
-                        rhs_scale=z_planes[e][:],
+                        rhs=z_codes[:, j0:j1].bitcast(FP8X4),
+                        rhs_scale=z_planes[:, j0:j1],
                         start=True,
                         stop=True,
                     )
-                res = sb("res%d_%d" % (e, g), [P, BANK], F32)
-                copy(out=res[:], in_=acc[:])
+                res = sb("res%d_%d" % (j0, g), [P, blocks * width], F32)
+                copy(out=res[:], in_=acc[:, 0 : blocks * width])
                 nc.sync.dma_start(
-                    out=out[2 * g * P : 2 * (g + 1) * P, e * HALF : (e + 1) * HALF].rearrange("(s p) j -> p s j", p=P),
-                    in_=res[:].rearrange("p (s j) -> p s j", s=2),
+                    out=out[blocks * g * P : blocks * (g + 1) * P, j0:j1].rearrange("(s p) j -> p s j", p=P),
+                    in_=res[:].rearrange("p (s j) -> p s j", s=blocks),
                 )
 
         on_scalar, on_vector = nc.scalar.copy, nc.vector.tensor_copy
-        for a in range(LAST):
+        gather_words(LAST, 0, BANK)
+        gather_words(LAST, BANK, S)
+        gain_sb = [placed("gain%d" % t, [P, 1], F32, 4 * T * LAST + 64 * t) for t in range(PACK)]
+        gain_low = gain.rearrange("(t b g j o) -> g t b j o", t=2, g=2, j=8, o=1)[0]
+        gain_high = gain.rearrange("(b g t i o) -> g t b i o", g=2, t=2, i=4, o=1)[1]
+        with nc.allow_non_contiguous_dma(reason="one gain to a partition"):
             for t in range(PACK):
-                round_w1(a, t, on_vector if a == 1 and t < 2 else on_scalar)
-            quantise_w1(a)
+                nc.sync.dma_start(out=gain_sb[t][:], in_=(gain_low if t < 2 else gain_high)[t % 2])
+        w2_raw = placed("w2_raw", [P, PACK, N], F32, 4 * T * LAST + 64 * PACK)
+        nc.sync.dma_start(
+            out=w2_raw[:, 0:2, :].rearrange("p t n -> p (t n)"),
+            in_=w2.rearrange("(b g i t) n -> g b i (t n)", g=2, i=4, t=2)[0],
+        )
+        w2_high = w2.rearrange("(b g t i) n -> g t b i n", g=2, t=2, i=4)[1]
+        for t in range(2):
+            nc.sync.dma_start(out=w2_raw[:, 2 + t, :], in_=w2_high[t])
+        for a in range(PASSES):
+            round_low(0, a, on_vector if a == LAST else on_scalar)
+            quantise_low(0, a)
+            if a < LAST:
+                round_high(0, a, on_vector if a else on_scalar)
+        round_high(0, LAST, on_vector)
+        gate_sums = product(0, "acc_a", wg_slice)
+        sigmoids(0, gate_sums)
+        make_h(0, product(0, "acc_x", w1_slice))
+        sigmoids(1, product(1, "acc_x", wg_slice))
+        second = [sb("second%d" % t, [P, PAIRS], F32) for t in range(3)]
+        factor = [sb("factor%d" % t, [P, PAIRS], F32) for t in range(2)]
+        z_low = [sb("z_low%d" % t, [P, PAIRS], F32) for t in range(2)]
+        pick_second(0, 0, PAIRS, second[0][:])
+        for a in range(PASSES):
+            round_low(1, a, on_vector if a == LAST else on_scalar)
+            quantise_low(1, a)
+        make_h(1, product(1, "acc_a", w1_slice))
+        for a in range(PASSES):
+            round_high(1, a, on_scalar)
+            quantise_high(a)
+        pick_second(1, 0, PAIRS, second[1][:])
+        bend(0, 0, PAIRS, second[0][:], factor[0][:])
+        pick_first(0, 0, PAIRS, factor[0][:], z_low[0][:])
+        move_low(0, z_low[0])
+        sigmoids(2, product(2, "acc_x", wg_slice))
+        make_h(2, product(2, "acc_y", w1_slice))
+        bend(1, 0, PAIRS, second[1][:], factor[1][:])
+        pick_first(1, 0, PAIRS, factor[1][:], z_low[1][:])
+        move_low(1, z_low[1])
+        pick_second(2, 0, PAIRS, second[2][:])
+        sigmoids(3, product(3, "acc_a", wg_slice))
+        make_h(3, product(3, "acc_b", w1_slice))
+        for m in range(N // P):
+            round_w2(m)
 
-        first_gate = product(0, "acc_a", wg_slice)
-        backs = placed("backs", [P, PACK + 1, BANK], F32, 3 * BANK_BYTES)
-        fronts = [placed("front%d" % t, [P, BANK], F32, BANK_BYTES * t) for t in range(PACK - 1)]
-        fronts.append(sb("front3", [P, BANK], F32))
-        gates = [(fronts[t][:], backs[:, t, :]) for t in range(PACK)]
-        z_front = backs[:, 1:, BANK - HALF :]
-        last_factor = in_turn("last_factor", [P, HALF], F32, "after_front")
-
-        round_w1(LAST, 0, on_vector)
-        sigmoids(0, first_gate)
-        quantise_last(0)
-        round_w1(LAST, 1, on_scalar)
-        make_h(0, "acc_x")
-        for t in range(1, PACK):
-            sigmoids(t, product(t, "acc_b" if t == 1 else "acc_x", wg_slice))
-            quantise_last(t)
-            if t + 1 < PACK:
-                round_w1(LAST, t + 1, on_scalar)
-            pick_second(t - 1, 0, PAIRS, factor[:, t - 1, :])
-            if t > 1:
-                pick_first(t - 2, 0, HALF, factor[:, t - 2, 0:HALF], z_front[:, t - 2, :])
-            if t + 1 == PACK:
-                for m in range(N // P):
-                    round_w2(m)
-            make_h(t, "acc_y")
-
-        end = PACK - 1
-        pick_second(end, 0, HALF, last_factor[:])
-        pick_first(end - 1, 0, HALF, factor[:, end - 1, 0:HALF], z_front[:, end - 1, :])
-        pick_second(end, HALF, PAIRS, factor[:, end, HALF:PAIRS])
+        front_factor = [in_turn("front_factor%d" % t, [P, HALF], F32, "after_front%d" % t) for t in range(2)]
+        back_factor = [sb("back_factor%d" % t, [P, HALF], F32) for t in range(2)]
+        last_second = sb("last_second", [P, HALF], F32)
+        bend(2, 0, HALF, second[2][:, 0:HALF], front_factor[0][:])
+        pick_second(3, 0, HALF, last_second[:])
+        bend(3, 0, HALF, last_second[:], front_factor[1][:])
+        for t in range(2):
+            pick_first(2 + t, 0, HALF, front_factor[t][:], z[0][:, (2 + t) * HALF : (3 + t) * HALF])
+        z_bf_front = z[1][:, 2 * HALF :].bitcast(BF16)
+        weave(0, HALF, z_bf_front, on_scalar)
+        back_second = in_turn("back_second", [P, HALF], F32, "after_front1")
+        pick_second(3, HALF, PAIRS, back_second[:])
+        w2_codes = in_turn("w2_codes", [P, N], U32, "after_front0")
         quantise_w2(0, 4)
-        pick_first(end, 0, HALF, last_factor[:], z_front[:, end, :])
-        z_back = in_turn("z_back", [P, PACK * HALF], F32, "after_front")
-        z_bf_front = z_back[:, 2 * HALF :].bitcast(BF16)
-        weave(z_front, z_bf_front, on_scalar)
         quantise_w2(4, 6)
-        for t in range(PACK):
-            pick_first(t, HALF, PAIRS, factor[:, t, HALF:PAIRS], z_back[:, HALF * t : HALF * (t + 1)])
-            if t == 1:
-                quantise_z(0, z_bf_front)
-                project(0, [on_scalar] * 3)
-        weave(z_back[:].rearrange("p (t j) -> p t j", t=PACK), z_bf_back[:], on_vector)
-        quantise_z(1, z_bf_back[:])
-        project(1, [on_vector, on_scalar, on_vector])
+        bend(2, HALF, PAIRS, second[2][:, HALF:], back_factor[0][:])
+        bend(3, HALF, PAIRS, back_second[:], back_factor[1][:])
+        quantise_z(0, HALF, z_bf_front)
+        project(0, HALF, ["acc_x", "acc_y", "acc_x"], [on_scalar] * 3)
+        QUARTER = HALF // 2
+        pick_first(2, HALF, PAIRS, back_factor[0][:], z[1][:, 2 * HALF : 3 * HALF])
+        woven = [sb("woven%d" % c, [P, QUARTER * PACK], BF16) for c in range(2)]
+        for c in range(2):
+            j0 = HALF + c * QUARTER
+            cols = slice(c * QUARTER, (c + 1) * QUARTER)
+            pick_first(3, j0, j0 + QUARTER, back_factor[1][:, cols], z[1][:, 3 * HALF :][:, cols])
+        for c in range(2):
+            j0 = HALF + c * QUARTER
+            weave(j0, j0 + QUARTER, woven[c][:], on_vector)
+        for c in range(2):
+            j0 = HALF + c * QUARTER
+            quantise_z(j0, j0 + QUARTER, woven[c][:])
+        project(HALF, HALF + QUARTER, ["acc_y", "acc_a"], [on_vector, on_scalar])
+        project(HALF + QUARTER, PAIRS, ["acc_b", "acc_a"], [on_vector, on_scalar])

@@ -24,7 +24,6 @@ BANK = 512
 HALF = PAIRS // 2
 SIDE = H // 2
 SCALE_ROWS = 16 * PASSES
-PLANE = S + H
 ROW0 = 48
 
 
@@ -50,31 +49,34 @@ def tile_list_fused_passage_pairs_kernel(
         pos1_sb = keep.tile([P, PAIRS // 16], U16, name="pos1_sb")
         pos2_sb = keep.tile([P, PAIRS // 16], U16, name="pos2_sb")
 
-        scale_rows = sb("scale_rows", [P, T], U8)
-        wg_scale_rows = sb("wg_scale_rows", [P, H], U8)
-        planes = sb("planes", [P, PASSES * PLANE], U8)
-
-        def load_scales(rows, scales, queue):
-            for a in range(PASSES):
-                queue.dma_start(
-                    out=rows[ROW0 + a : ROW0 + SCALE_ROWS : PASSES, :].bitcast(I32), in_=scales.bitcast(I32)[a]
-                )
+        RAW = 4 * PACK * SIDE
+        WG = PASSES * SIDE * 2
+        TABLE_AT = [RAW // 2, 3 * RAW + WG + RAW // 2, 6 * RAW + WG]
+        W1_AT = {(0, 0): 0, (0, 1): RAW + WG, (0, 2): 2 * RAW + WG}
+        for a in range(PASSES):
+            W1_AT[1, a] = (3 + a) * RAW + WG
+        GATE1_AT = TABLE_AT[LAST] + 64 * PACK + 4 * PACK * N
+        scale_rows = placed("scale_rows", [P, T], U8, TABLE_AT[LAST])
+        wg_scale_rows = sb("wg_scale_rows", [P, PASSES * H], U8)
+        planes = sb("planes", [P, PASSES * S], U8)
 
         nc.sync.dma_start(offs_sb[:], offs)
-        load_scales(scale_rows, tab_scales, nc.sync)
-        load_scales(wg_scale_rows, wg_scales, nc.scalar)
-        for rows in (scale_rows, wg_scale_rows):
-            nc.vector.memset(rows[0:ROW0, :].bitcast(I32), 0)
-            nc.vector.memset(rows[ROW0 + SCALE_ROWS :, :].bitcast(I32), 0)
+        for a in range(PASSES):
+            rows = scale_rows[ROW0 + a : ROW0 + 32 : 2, :] if a < LAST else scale_rows[ROW0 + 32 : ROW0 + SCALE_ROWS, :]
+            nc.sync.dma_start(out=rows.bitcast(I32), in_=tab_scales.bitcast(I32)[a])
+        nc.vector.memset(scale_rows[0:ROW0, :].bitcast(I32), 0)
+        nc.vector.memset(scale_rows[ROW0 + SCALE_ROWS :, :].bitcast(I32), 0)
+        nc.vector.memset(wg_scale_rows[:].bitcast(I32), 0)
         nc.vector.memset(planes[:].bitcast(I32), 0)
 
         warm = sb("warm", [P, 2], F32)
         nc.vector.memset(warm[:, 0:1], 0.0)
         nc.scalar.activation(warm[:, 1:2], warm[:, 0:1], ACT.Sigmoid)
 
-        table = [placed("table%d" % a, [P, T], U32, 4 * T * a) for a in range(PASSES)]
+        table = {}
 
         def load_table(a):
+            table[a] = placed("table%d" % a, [P, T], U32, TABLE_AT[a])
             nc.sync.dma_start(
                 out=table[a][:].bitcast(I32),
                 in_=tab_words[a].rearrange("p t i -> p (t i)").bitcast(I32),
@@ -82,57 +84,74 @@ def tile_list_fused_passage_pairs_kernel(
 
         w1_raw = {}
 
-        def load_w1(side, a, place, where):
-            w1_raw[side, a] = place("w1_raw%d_%d" % (side, a), [P, PACK, SIDE], F32, where)
+        def load_w1(side, a):
+            w1_raw[side, a] = placed("w1_raw%d_%d" % (side, a), [P, PACK, SIDE], F32, W1_AT[side, a])
             rows = w1[512 * a : 512 * (a + 1), side * SIDE : (side + 1) * SIDE]
             nc.sync.dma_start(out=w1_raw[side, a][:], in_=rows.rearrange("(p j) c -> p j c", j=PACK))
 
+        def load_wg(side, raw):
+            words = wg_words.bitcast(I32).rearrange("a p e -> p a e")
+            nc.sync.dma_start(out=raw[:], in_=words[:, :, side * SIDE // 2 : (side + 1) * SIDE // 2])
+
         load_table(0)
+        for q in range(4):
+            nc.sync.dma_start(
+                out=wg_scale_rows[32 * q : 32 * q + 4, :].bitcast(I32).rearrange("r (a c) -> r a c", a=PASSES),
+                in_=wg_scales.bitcast(I32)[:, 4 * q : 4 * q + 4, :].rearrange("a r c -> r a c"),
+            )
+        wg_raw = [sb("wg_raw0", [P, PASSES, SIDE // 2], I32)]
+        load_wg(0, wg_raw[0])
+        load_table(1)
         nc.sync.dma_start(pos2_sb[:], pos2)
         nc.sync.dma_start(pos1_sb[:], pos1)
-        wg_raw = in_turn("wg_raw", [P, PASSES, H // 2], I32, "after_wg")
-        nc.sync.dma_start(out=wg_raw[:], in_=wg_words.bitcast(I32).rearrange("a p e -> p a e"))
-        load_table(1)
-        load_table(LAST)
 
         picked_rows = sb("picked_rows", [P, S], U8)
         nc.vector.tensor_copy(picked_rows[:], scale_rows[:].indirect(offs_sb[:]))
-        both_rows = in_turn("both_rows", [P, PLANE], U8, "after_moves")
-        nc.vector.tensor_copy(both_rows[:, 0:S].bitcast(I32), picked_rows[:].bitcast(I32))
-        by_block = wg_scale_rows[:].bitcast(I32).rearrange("p (b g w) -> p g b w", g=2, w=2)
-        nc.vector.tensor_copy(
-            out=both_rows[:, S : S + SIDE].bitcast(I32).rearrange("p (b w) -> p b w", w=2), in_=by_block[:, 0]
-        )
-        nc.vector.tensor_copy(
-            out=both_rows[:, S + SIDE :].bitcast(I32).rearrange("p (t b) -> p t b", t=2),
-            in_=by_block[:, 1].rearrange("p b t -> p t b"),
-        )
         for q in range(4):
-            (nc.scalar if q % 2 else nc.sync).dma_start(
-                out=planes[32 * q : 32 * q + 4, :].bitcast(I32).rearrange("r (a s) -> r a s", a=PASSES),
-                in_=both_rows[ROW0 + 12 * q : ROW0 + 12 * q + 12, :].bitcast(I32),
+            nc.sync.dma_start(
+                out=planes[32 * q : 32 * q + 4, 0 : 2 * S].bitcast(I32).rearrange("r (a s) -> r a s", a=2),
+                in_=picked_rows[ROW0 + 8 * q : ROW0 + 8 * q + 8, :].bitcast(I32),
             )
+        load_table(LAST)
+        for q in range(4):
+            nc.sync.dma_start(
+                out=planes[32 * q : 32 * q + 4, 2 * S :].bitcast(I32),
+                in_=picked_rows[ROW0 + 32 + 4 * q : ROW0 + 32 + 4 * q + 4, :].bitcast(I32),
+            )
+        wg_planes = sb("wg_planes", [P, PASSES * H], U8)
+        dealt = wg_planes[:].bitcast(U32).rearrange("p (a g c) -> p g a c", a=PASSES, g=2)
+        by_block = wg_scale_rows[:].bitcast(U32).rearrange("p (a b g w) -> p g a b w", a=PASSES, g=2, w=2)
+        nc.scalar.copy(out=dealt[:, 0].rearrange("p a (b w) -> p a b w", w=2), in_=by_block[:, 0])
+        nc.scalar.copy(
+            out=dealt[:, 1].rearrange("p a (t b) -> p a t b", t=2), in_=by_block[:, 1].rearrange("p a b t -> p a t b")
+        )
+        wg_low = [sb("wg_low%d" % t, [P, PASSES * 2 * P], U8) for t in range(2)]
+        wg_high = sb("wg_high", [P, PASSES * 4 * P], U8)
+
+        def deal_wg(side):
+            by_block = wg_raw[side][:].bitcast(U32).rearrange("p a (b g w) -> p g a b w", g=2, w=4)
+            nc.scalar.copy(
+                out=wg_low[side][:].bitcast(U32).rearrange("p (a b w) -> p a b w", a=PASSES, w=4), in_=by_block[:, 0]
+            )
+            nc.scalar.copy(
+                out=wg_high[:].bitcast(U32).rearrange("p (a t s b w) -> p s a t b w", a=PASSES, t=2, s=2, w=2)[:, side],
+                in_=by_block[:, 1].rearrange("p a b (t w) -> p a t b w", t=2),
+            )
+
+        deal_wg(0)
         v_words = [sb("v_words%d" % a, [P, S], U32) for a in range(PASSES)]
 
         def gather_words(a, s0, s1):
             nc.vector.tensor_copy(v_words[a][:, s0:s1], table[a][:].indirect(offs_sb[:, s0 // 16 : s1 // 16]))
 
         gather_words(0, 0, S)
-        for a in range(LAST):
-            load_w1(0, a, placed, 2 * T * a)
-        wg_codes = sb("wg_codes", [P, PASSES * 2 * H], U8)
-        dealt = wg_codes[:].bitcast(I32).rearrange("p (a g c) -> p g a c", a=PASSES, g=2)
-        by_block = wg_raw[:].rearrange("p a (b g w) -> p g a b w", g=2, w=4)
-        nc.vector.tensor_copy(out=dealt[:, 0].rearrange("p a (b w) -> p a b w", w=4), in_=by_block[:, 0])
-        nc.vector.tensor_copy(
-            out=dealt[:, 1].rearrange("p a (t b w) -> p a t b w", t=2, w=2),
-            in_=by_block[:, 1].rearrange("p a b (t w) -> p a t b w", t=2),
-        )
-        load_w1(0, LAST, in_turn, "after_wg")
-        load_w1(1, 0, in_turn, "after_moves")
+        for a in range(PASSES):
+            load_w1(0, a)
+        wg_raw.append(placed("wg_raw1", [P, PASSES, SIDE // 2], I32, RAW))
+        load_wg(1, wg_raw[1])
         gather_words(1, 0, S)
-        for a in range(1, PASSES):
-            load_w1(1, a, placed, 2 * T * (a + 1))
+        for a in range(PASSES):
+            load_w1(1, a)
 
         low_bf, high_bf = {}, {}
         low_codes = [sb("low_codes%d" % t, [P, PASSES * P], U32) for t in range(2)]
@@ -141,7 +160,11 @@ def tile_list_fused_passage_pairs_kernel(
         high_planes = [sb("high_planes%d" % a, [P, 2 * P], U8) for a in range(PASSES)]
 
         def round_low(side, a, copy):
-            low_bf[side, a] = in_turn("low_bf%d_%d" % (side, a), [P, H], BF16, "low_bf%d_%d" % (side, a))
+            name = "low_bf%d_%d" % (side, a)
+            if (side, a) == (1, LAST):
+                low_bf[side, a] = placed(name, [P, H], BF16, GATE1_AT + 4 * BANK - H)
+            else:
+                low_bf[side, a] = in_turn(name, [P, H], BF16, name)
             copy(
                 out=low_bf[side, a][:].rearrange("p (b f i j) -> p b f j i", f=2, i=4, j=PACK),
                 in_=w1_raw[side, a][:].rearrange("p j (b g f i) -> p g b f j i", g=2, f=2, i=4)[:, 0],
@@ -176,16 +199,17 @@ def tile_list_fused_passage_pairs_kernel(
                         lhsT=codes,
                         lhsT_scale=scales,
                         rhs=v_words[a][:, u * BANK : (u + 1) * BANK].bitcast(FP8X4),
-                        rhs_scale=planes[:, a * PLANE + u * BANK : a * PLANE + (u + 1) * BANK],
+                        rhs_scale=planes[:, a * S + u * BANK : a * S + (u + 1) * BANK],
                         start=(a == 0),
                         stop=(a == LAST),
                     )
             return accs
 
         def wg_slice(a, t):
-            col = a * H + t * P
-            first = a * PLANE + S + t * P
-            return wg_codes[:, 2 * col : 2 * (col + P)].bitcast(FP4X4), planes[:, first : first + P]
+            col = a * P if t < 2 else (2 * a + t - 2) * P
+            codes = wg_low[t] if t < 2 else wg_high
+            first = a * H + t * P
+            return codes[:, 2 * col : 2 * (col + P)].bitcast(FP4X4), wg_planes[:, first : first + P]
 
         def w1_slice(a, t):
             if t < 2:
@@ -198,27 +222,30 @@ def tile_list_fused_passage_pairs_kernel(
         def sigmoids(t, accs):
             for u, acc in enumerate(accs):
                 name = "gate%d_%d" % (t, u)
-                gates[t, u] = sb(name, [P, BANK], F32) if t else placed(name, [P, BANK], F32, 2 * T * u)
+                if t < 2:
+                    gates[t, u] = placed(name, [P, BANK], F32, GATE1_AT + 4 * BANK * u if t else W1_AT[0, u])
+                else:
+                    gates[t, u] = in_turn(name, [P, BANK], F32, name)
                 nc.scalar.activation(gates[t, u][:], acc[:], ACT.Sigmoid)
 
-        w2_bf = sb("w2_bf", [P, N * PACK], BF16)
+        w2_bf = {}
         w2_planes = sb("w2_planes", [P, N], U8)
 
-        def round_w2(m):
-            nc.scalar.copy(
-                out=w2_bf[:, m * P * PACK : (m + 1) * P * PACK].rearrange("p (c i t) -> p c t i", i=4, t=PACK),
-                in_=w2_raw[:, :, m * P : (m + 1) * P].rearrange("p t (c i) -> p c t i", i=4),
+        def round_w2(m0, m1, dest, copy):
+            copy(
+                out=dest.rearrange("p (c i t) -> p c t i", i=4, t=PACK),
+                in_=w2_raw[:, :, m0 * P : m1 * P].rearrange("p t (c i) -> p c t i", i=4),
             )
 
         def quantise_w2(m0, m1):
             nc.vector.quantize_mx(
                 out=w2_codes[:, m0 * P : m1 * P].bitcast(FP8X4),
                 scales=w2_planes[:, m0 * P : m1 * P],
-                in_=w2_bf[:, m0 * P * PACK : m1 * P * PACK],
+                in_=w2_bf[m0][:],
             )
 
         h = [sb("h%d" % t, [P, S], F32) for t in range(PACK)]
-        bent = sb("bent", [P, PACK, PAIRS], F32)
+        bent = {}
         z = [sb("z%d" % e, [P, PACK * HALF], F32) for e in range(2)]
         z_codes = sb("z_codes", [P, PAIRS], U32)
         z_planes = sb("z_planes", [P, PAIRS], U8)
@@ -232,8 +259,10 @@ def tile_list_fused_passage_pairs_kernel(
             nc.vector.tensor_copy(dest, h[t][:].indirect(pos2_sb[:, j0 // 16 : j1 // 16]))
 
         def bend(t, j0, j1, second, dest):
-            nc.scalar.activation(bent[:, t, j0:j1], second, ACT.Tanh)
-            nc.scalar.activation(dest, bent[:, t, j0:j1], ACT.Copy, scale=gain_sb[t][:])
+            name = "bent%d_%d" % (t, j0)
+            bent[t, j0] = sb(name, [P, j1 - j0], F32) if t else placed(name, [P, PAIRS], F32, GATE1_AT)
+            nc.scalar.activation(bent[t, j0][:], second, ACT.Tanh)
+            nc.scalar.activation(dest, bent[t, j0][:], ACT.Copy, scale=gain_sb[t][:])
 
         def pick_first(t, j0, j1, other, dest):
             nc.vector.tensor_tensor(dest, h[t][:].indirect(pos1_sb[:, j0 // 16 : j1 // 16]), other, MULT)
@@ -281,13 +310,13 @@ def tile_list_fused_passage_pairs_kernel(
         on_scalar, on_vector = nc.scalar.copy, nc.vector.tensor_copy
         gather_words(LAST, 0, BANK)
         gather_words(LAST, BANK, S)
-        gain_sb = [placed("gain%d" % t, [P, 1], F32, 4 * T * LAST + 64 * t) for t in range(PACK)]
+        gain_sb = [placed("gain%d" % t, [P, 1], F32, TABLE_AT[LAST] + 64 * t) for t in range(PACK)]
         gain_low = gain.rearrange("(t b g j o) -> g t b j o", t=2, g=2, j=8, o=1)[0]
         gain_high = gain.rearrange("(b g t i o) -> g t b i o", g=2, t=2, i=4, o=1)[1]
         with nc.allow_non_contiguous_dma(reason="one gain to a partition"):
             for t in range(PACK):
                 nc.sync.dma_start(out=gain_sb[t][:], in_=(gain_low if t < 2 else gain_high)[t % 2])
-        w2_raw = placed("w2_raw", [P, PACK, N], F32, 4 * T * LAST + 64 * PACK)
+        w2_raw = placed("w2_raw", [P, PACK, N], F32, TABLE_AT[LAST] + 64 * PACK)
         nc.sync.dma_start(
             out=w2_raw[:, 0:2, :].rearrange("p t n -> p (t n)"),
             in_=w2.rearrange("(b g i t) n -> g b i (t n)", g=2, i=4, t=2)[0],
@@ -299,39 +328,49 @@ def tile_list_fused_passage_pairs_kernel(
             round_low(0, a, on_vector if a == LAST else on_scalar)
             quantise_low(0, a)
             if a < LAST:
-                round_high(0, a, on_vector if a else on_scalar)
+                round_high(0, a, on_scalar)
         round_high(0, LAST, on_vector)
         gate_sums = product(0, "acc_a", wg_slice)
         sigmoids(0, gate_sums)
         make_h(0, product(0, "acc_x", w1_slice))
-        sigmoids(1, product(1, "acc_x", wg_slice))
-        second = [sb("second%d" % t, [P, PAIRS], F32) for t in range(3)]
+        deal_wg(1)
+        second = {}
         factor = [sb("factor%d" % t, [P, PAIRS], F32) for t in range(2)]
-        z_low = [sb("z_low%d" % t, [P, PAIRS], F32) for t in range(2)]
-        pick_second(0, 0, PAIRS, second[0][:])
         for a in range(PASSES):
-            round_low(1, a, on_vector if a == LAST else on_scalar)
+            round_low(1, a, on_scalar)
             quantise_low(1, a)
-        make_h(1, product(1, "acc_a", w1_slice))
+        second[0] = in_turn("second0", [P, PAIRS], F32, "low_bf1_0")
+        pick_second(0, 0, PAIRS, second[0][:])
+        sigmoids(1, product(1, "acc_y", wg_slice))
+        make_h(1, product(1, "acc_b", w1_slice))
         for a in range(PASSES):
             round_high(1, a, on_scalar)
             quantise_high(a)
+        second[1] = in_turn("second1", [P, PAIRS], F32, "low_bf0_%d" % LAST)
         pick_second(1, 0, PAIRS, second[1][:])
         bend(0, 0, PAIRS, second[0][:], factor[0][:])
+        z_low = [sb("z_low0", [P, PAIRS], F32)]
         pick_first(0, 0, PAIRS, factor[0][:], z_low[0][:])
         move_low(0, z_low[0])
-        sigmoids(2, product(2, "acc_x", wg_slice))
-        make_h(2, product(2, "acc_y", w1_slice))
+        sigmoids(2, product(2, "acc_y", wg_slice))
+        make_h(2, product(2, "acc_b", w1_slice))
         bend(1, 0, PAIRS, second[1][:], factor[1][:])
+        second[2] = sb("second2", [P, PAIRS], F32)
+        pick_second(2, 0, PAIRS, second[2][:])
+        z_low.append(in_turn("z_low1", [P, PAIRS], F32, "gate2_1"))
         pick_first(1, 0, PAIRS, factor[1][:], z_low[1][:])
         move_low(1, z_low[1])
-        pick_second(2, 0, PAIRS, second[2][:])
-        sigmoids(3, product(3, "acc_a", wg_slice))
+        sigmoids(3, product(3, "acc_y", wg_slice))
         make_h(3, product(3, "acc_b", w1_slice))
-        for m in range(N // P):
-            round_w2(m)
+        w2_bf[0] = sb("w2_bf0", [P, 4 * P * PACK], BF16)
+        for m in range(4):
+            round_w2(m, m + 1, w2_bf[0][:, m * P * PACK : (m + 1) * P * PACK], on_scalar)
 
-        front_factor = [in_turn("front_factor%d" % t, [P, HALF], F32, "after_front%d" % t) for t in range(2)]
+        END = GATE1_AT + 8 * BANK
+        front_factor = [
+            in_turn("front_factor0", [P, HALF], F32, "after_front0"),
+            placed("front_factor1", [P, HALF], F32, END + 2 * HALF),
+        ]
         back_factor = [sb("back_factor%d" % t, [P, HALF], F32) for t in range(2)]
         last_second = sb("last_second", [P, HALF], F32)
         bend(2, 0, HALF, second[2][:, 0:HALF], front_factor[0][:])
@@ -339,17 +378,19 @@ def tile_list_fused_passage_pairs_kernel(
         bend(3, 0, HALF, last_second[:], front_factor[1][:])
         for t in range(2):
             pick_first(2 + t, 0, HALF, front_factor[t][:], z[0][:, (2 + t) * HALF : (3 + t) * HALF])
+        w2_bf[4] = in_turn("w2_bf4", [P, 2 * P * PACK], BF16, "after_front0")
+        round_w2(4, 6, w2_bf[4][:], on_vector)
         z_bf_front = z[1][:, 2 * HALF :].bitcast(BF16)
         weave(0, HALF, z_bf_front, on_scalar)
-        back_second = in_turn("back_second", [P, HALF], F32, "after_front1")
+        back_second = placed("back_second", [P, HALF], F32, END)
         pick_second(3, HALF, PAIRS, back_second[:])
-        w2_codes = in_turn("w2_codes", [P, N], U32, "after_front0")
+        w2_codes = placed("w2_codes", [P, N], U32, END + 4 * HALF)
         quantise_w2(0, 4)
         quantise_w2(4, 6)
         bend(2, HALF, PAIRS, second[2][:, HALF:], back_factor[0][:])
         bend(3, HALF, PAIRS, back_second[:], back_factor[1][:])
         quantise_z(0, HALF, z_bf_front)
-        project(0, HALF, ["acc_x", "acc_y", "acc_x"], [on_scalar] * 3)
+        project(0, HALF, ["acc_x", "acc_a", "acc_x"], [on_scalar] * 3)
         QUARTER = HALF // 2
         pick_first(2, HALF, PAIRS, back_factor[0][:], z[1][:, 2 * HALF : 3 * HALF])
         woven = [sb("woven%d" % c, [P, QUARTER * PACK], BF16) for c in range(2)]
@@ -363,5 +404,5 @@ def tile_list_fused_passage_pairs_kernel(
         for c in range(2):
             j0 = HALF + c * QUARTER
             quantise_z(j0, j0 + QUARTER, woven[c][:])
-        project(HALF, HALF + QUARTER, ["acc_y", "acc_a"], [on_vector, on_scalar])
-        project(HALF + QUARTER, PAIRS, ["acc_b", "acc_a"], [on_vector, on_scalar])
+        project(HALF, HALF + QUARTER, ["acc_a", "acc_y"], [on_vector, on_scalar])
+        project(HALF + QUARTER, PAIRS, ["acc_b", "acc_y"], [on_vector, on_scalar])

@@ -245,7 +245,6 @@ def tile_list_fused_passage_pairs_kernel(
             )
 
         h = [sb("h%d" % t, [P, S], F32) for t in range(PACK)]
-        bent = {}
         z = [sb("z%d" % e, [P, PACK * HALF], F32) for e in range(2)]
         z_codes = sb("z_codes", [P, PAIRS], U32)
         z_planes = sb("z_planes", [P, PAIRS], U8)
@@ -259,13 +258,12 @@ def tile_list_fused_passage_pairs_kernel(
             nc.vector.tensor_copy(dest, h[t][:].indirect(pos2_sb[:, j0 // 16 : j1 // 16]))
 
         def bend(t, j0, j1, second, dest):
-            name = "bent%d_%d" % (t, j0)
-            bent[t, j0] = sb(name, [P, j1 - j0], F32) if t else placed(name, [P, PAIRS], F32, GATE1_AT)
-            nc.scalar.activation(bent[t, j0][:], second, ACT.Tanh)
-            nc.scalar.activation(dest, bent[t, j0][:], ACT.Copy, scale=gain_sb[t][:])
+            nc.scalar.activation(dest, second, ACT.Tanh)
 
         def pick_first(t, j0, j1, other, dest):
-            nc.vector.tensor_tensor(dest, h[t][:].indirect(pos1_sb[:, j0 // 16 : j1 // 16]), other, MULT)
+            first = sb("first%d_%d" % (t, j0), [P, j1 - j0], F32)
+            nc.vector.tensor_copy(first[:], h[t][:].indirect(pos1_sb[:, j0 // 16 : j1 // 16]))
+            nc.vector.scalar_tensor_tensor(dest, first[:], gain_sb[t][:], other, MULT, MULT)
 
         def move_low(t, z_low):
             for e in range(2):
@@ -335,7 +333,6 @@ def tile_list_fused_passage_pairs_kernel(
         make_h(0, product(0, "acc_x", w1_slice))
         deal_wg(1)
         second = {}
-        factor = [sb("factor%d" % t, [P, PAIRS], F32) for t in range(2)]
         for a in range(PASSES):
             round_low(1, a, on_scalar)
             quantise_low(1, a)
@@ -348,6 +345,7 @@ def tile_list_fused_passage_pairs_kernel(
             quantise_high(a)
         second[1] = in_turn("second1", [P, PAIRS], F32, "low_bf0_%d" % LAST)
         pick_second(1, 0, PAIRS, second[1][:])
+        factor = [placed("factor0", [P, PAIRS], F32, GATE1_AT), sb("factor1", [P, PAIRS], F32)]
         bend(0, 0, PAIRS, second[0][:], factor[0][:])
         z_low = [sb("z_low0", [P, PAIRS], F32)]
         pick_first(0, 0, PAIRS, factor[0][:], z_low[0][:])
@@ -378,8 +376,8 @@ def tile_list_fused_passage_pairs_kernel(
         bend(3, 0, HALF, last_second[:], front_factor[1][:])
         for t in range(2):
             pick_first(2 + t, 0, HALF, front_factor[t][:], z[0][:, (2 + t) * HALF : (3 + t) * HALF])
-        w2_bf[4] = in_turn("w2_bf4", [P, 2 * P * PACK], BF16, "after_front0")
-        round_w2(4, 6, w2_bf[4][:], on_vector)
+        w2_bf[4] = sb("w2_bf4", [P, 2 * P * PACK], BF16)
+        round_w2(4, 6, w2_bf[4][:], on_scalar)
         z_bf_front = z[1][:, 2 * HALF :].bitcast(BF16)
         weave(0, HALF, z_bf_front, on_scalar)
         back_second = placed("back_second", [P, HALF], F32, END)

@@ -22,7 +22,7 @@ PASSES = K // (P * PACK)
 LAST = PASSES - 1
 BANK = 512
 HALF = PAIRS // 2
-SIDE = H // 2
+QUARTER = PAIRS // 4
 SCALE_ROWS = 16 * PASSES
 ROW0 = 48
 
@@ -34,28 +34,23 @@ def tile_list_fused_passage_pairs_kernel(
     with ExitStack() as ctx:
         keep = ctx.enter_context(tc.tile_pool(name="keep", bufs=1))
         shared = ctx.enter_context(tc.tile_pool(name="shared", bufs=1))
-        psum = ctx.enter_context(tc.psum_pool(name="psum", bufs=2))
+        psum = ctx.enter_context(tc.psum_pool(name="psum", bufs=1))
 
-        def sb(name, shape, dtype):
-            return keep.tile(shape, dtype, name=name, align_bytes=64)
-
-        def in_turn(name, shape, dtype, tag):
-            return keep.tile(shape, dtype, name=name, tag=tag, align_bytes=64)
+        def sb(name, shape, dtype, tag=None):
+            return keep.tile(shape, dtype, name=name, tag=tag or name, align_bytes=64)
 
         def placed(name, shape, dtype, offset):
             return shared.tile(shape, dtype, name=name, offset=offset, align_bytes=64)
+
+        def bank(number):
+            return psum.tile([P, BANK], F32, name="bank%d" % number)
 
         offs_sb = keep.tile([P, S // 16], U16, name="offs_sb")
         pos1_sb = keep.tile([P, PAIRS // 16], U16, name="pos1_sb")
         pos2_sb = keep.tile([P, PAIRS // 16], U16, name="pos2_sb")
 
-        RAW = 4 * PACK * SIDE
-        WG = PASSES * SIDE * 2
-        TABLE_AT = [RAW // 2, 3 * RAW + WG + RAW // 2, 6 * RAW + WG]
-        W1_AT = {(0, 0): 0, (0, 1): RAW + WG, (0, 2): 2 * RAW + WG}
-        for a in range(PASSES):
-            W1_AT[1, a] = (3 + a) * RAW + WG
-        GATE1_AT = TABLE_AT[LAST] + 64 * PACK + 4 * PACK * N
+        RAW = 4 * PACK * H
+        TABLE_AT = [RAW // 2, 2 * RAW, 3 * RAW]
         scale_rows = placed("scale_rows", [P, T], U8, TABLE_AT[LAST])
         wg_scale_rows = sb("wg_scale_rows", [P, PASSES * H], U8)
         planes = sb("planes", [P, PASSES * S], U8)
@@ -84,14 +79,9 @@ def tile_list_fused_passage_pairs_kernel(
 
         w1_raw = {}
 
-        def load_w1(side, a):
-            w1_raw[side, a] = placed("w1_raw%d_%d" % (side, a), [P, PACK, SIDE], F32, W1_AT[side, a])
-            rows = w1[512 * a : 512 * (a + 1), side * SIDE : (side + 1) * SIDE]
-            nc.sync.dma_start(out=w1_raw[side, a][:], in_=rows.rearrange("(p j) c -> p j c", j=PACK))
-
-        def load_wg(side, raw):
-            words = wg_words.bitcast(I32).rearrange("a p e -> p a e")
-            nc.sync.dma_start(out=raw[:], in_=words[:, :, side * SIDE // 2 : (side + 1) * SIDE // 2])
+        def load_w1(a):
+            w1_raw[a] = placed("w1_raw%d" % a, [P, PACK, H], F32, a * RAW)
+            nc.sync.dma_start(out=w1_raw[a][:], in_=w1[512 * a : 512 * (a + 1), :].rearrange("(p j) c -> p j c", j=PACK))
 
         load_table(0)
         for q in range(4):
@@ -99,8 +89,8 @@ def tile_list_fused_passage_pairs_kernel(
                 out=wg_scale_rows[32 * q : 32 * q + 4, :].bitcast(I32).rearrange("r (a c) -> r a c", a=PASSES),
                 in_=wg_scales.bitcast(I32)[:, 4 * q : 4 * q + 4, :].rearrange("a r c -> r a c"),
             )
-        wg_raw = [sb("wg_raw0", [P, PASSES, SIDE // 2], I32)]
-        load_wg(0, wg_raw[0])
+        wg_raw = sb("wg_raw", [P, PASSES, H // 2], I32)
+        nc.sync.dma_start(out=wg_raw[:], in_=wg_words.bitcast(I32).rearrange("a p e -> p a e"))
         load_table(1)
         nc.sync.dma_start(pos2_sb[:], pos2)
         nc.sync.dma_start(pos1_sb[:], pos1)
@@ -118,175 +108,166 @@ def tile_list_fused_passage_pairs_kernel(
                 out=planes[32 * q : 32 * q + 4, 2 * S :].bitcast(I32),
                 in_=picked_rows[ROW0 + 32 + 4 * q : ROW0 + 32 + 4 * q + 4, :].bitcast(I32),
             )
+
         wg_planes = sb("wg_planes", [P, PASSES * H], U8)
-        dealt = wg_planes[:].bitcast(U32).rearrange("p (a g c) -> p g a c", a=PASSES, g=2)
-        by_block = wg_scale_rows[:].bitcast(U32).rearrange("p (a b g w) -> p g a b w", a=PASSES, g=2, w=2)
-        nc.scalar.copy(out=dealt[:, 0].rearrange("p a (b w) -> p a b w", w=2), in_=by_block[:, 0])
         nc.scalar.copy(
-            out=dealt[:, 1].rearrange("p a (t b) -> p a t b", t=2), in_=by_block[:, 1].rearrange("p a b t -> p a t b")
+            out=wg_planes[:].bitcast(U32).rearrange("p (a t g) -> p a t g", a=PASSES, t=PACK),
+            in_=wg_scale_rows[:].bitcast(U32).rearrange("p (a g t) -> p a t g", a=PASSES, t=PACK),
         )
-        wg_low = [sb("wg_low%d" % t, [P, PASSES * 2 * P], U8) for t in range(2)]
-        wg_high = sb("wg_high", [P, PASSES * 4 * P], U8)
+        wg_codes = sb("wg_codes", [P, PASSES * 2 * H], U8)
+        nc.scalar.copy(
+            out=wg_codes[:].bitcast(U32).rearrange("p (a t g w) -> p a t g w", a=PASSES, t=PACK, w=2),
+            in_=wg_raw[:].bitcast(U32).rearrange("p a (g t w) -> p a t g w", t=PACK, w=2),
+        )
 
-        def deal_wg(side):
-            by_block = wg_raw[side][:].bitcast(U32).rearrange("p a (b g w) -> p g a b w", g=2, w=4)
-            nc.scalar.copy(
-                out=wg_low[side][:].bitcast(U32).rearrange("p (a b w) -> p a b w", a=PASSES, w=4), in_=by_block[:, 0]
-            )
-            nc.scalar.copy(
-                out=wg_high[:].bitcast(U32).rearrange("p (a t s b w) -> p s a t b w", a=PASSES, t=2, s=2, w=2)[:, side],
-                in_=by_block[:, 1].rearrange("p a b (t w) -> p a t b w", t=2),
-            )
-
-        deal_wg(0)
         v_words = [sb("v_words%d" % a, [P, S], U32) for a in range(PASSES)]
 
         def gather_words(a, s0, s1):
             nc.vector.tensor_copy(v_words[a][:, s0:s1], table[a][:].indirect(offs_sb[:, s0 // 16 : s1 // 16]))
 
         gather_words(0, 0, S)
-        for a in range(PASSES):
-            load_w1(0, a)
-        wg_raw.append(placed("wg_raw1", [P, PASSES, SIDE // 2], I32, RAW))
-        load_wg(1, wg_raw[1])
+        load_w1(0)
+        load_w1(1)
         gather_words(1, 0, S)
-        for a in range(PASSES):
-            load_w1(1, a)
+        load_w1(LAST)
+        gather_words(LAST, 0, BANK)
+        gather_words(LAST, BANK, S)
+        gain_sb = [placed("gain%d" % t, [P, 1], F32, TABLE_AT[LAST] + 64 * t) for t in range(PACK)]
+        with nc.allow_non_contiguous_dma(reason="one gain to a partition"):
+            for t in range(PACK):
+                nc.sync.dma_start(out=gain_sb[t][:], in_=gain.rearrange("(g t i o) -> t g i o", t=PACK, i=4, o=1)[t])
+        w2_raw = placed("w2_raw", [P, PACK, N], F32, TABLE_AT[LAST] + 64 * PACK)
+        for t in range(PACK):
+            nc.sync.dma_start(out=w2_raw[:, t, :], in_=w2.rearrange("(g t i) n -> t g i n", t=PACK, i=4)[t])
 
-        low_bf, high_bf = {}, {}
-        low_codes = [sb("low_codes%d" % t, [P, PASSES * P], U32) for t in range(2)]
-        low_planes = [sb("low_planes%d" % t, [P, PASSES * P], U8) for t in range(2)]
-        high_codes = [sb("high_codes%d" % a, [P, 2 * P], U32) for a in range(PASSES)]
-        high_planes = [sb("high_planes%d" % a, [P, 2 * P], U8) for a in range(PASSES)]
-
-        def round_low(side, a, copy):
-            name = "low_bf%d_%d" % (side, a)
-            if (side, a) == (1, LAST):
-                low_bf[side, a] = placed(name, [P, H], BF16, GATE1_AT + 4 * BANK - H)
-            else:
-                low_bf[side, a] = in_turn(name, [P, H], BF16, name)
-            copy(
-                out=low_bf[side, a][:].rearrange("p (b f i j) -> p b f j i", f=2, i=4, j=PACK),
-                in_=w1_raw[side, a][:].rearrange("p j (b g f i) -> p g b f j i", g=2, f=2, i=4)[:, 0],
+        def first_stage_pass(acc, a, u, codes, scales, start, stop):
+            nc.tensor.matmul_mx(
+                out=acc[:],
+                lhsT=codes,
+                lhsT_scale=scales,
+                rhs=v_words[a][:, u * BANK : (u + 1) * BANK].bitcast(FP8X4),
+                rhs_scale=planes[:, a * S + u * BANK : a * S + (u + 1) * BANK],
+                start=start,
+                stop=stop,
             )
 
-        def round_high(side, a, copy):
-            if side == 0:
-                tag = "low_bf0_%d" % a if a == LAST else "high_bf%d" % a
-                high_bf[a] = in_turn("high_bf%d" % a, [P, 2 * H], BF16, tag)
-            copy(
-                out=high_bf[a][:].rearrange("p (t s b i j) -> p s t b j i", t=2, s=2, i=4, j=PACK)[:, side],
-                in_=w1_raw[side, a][:].rearrange("p j (b g t i) -> p g t b j i", g=2, t=2, i=4)[:, 1],
-            )
+        sums, gates = {}, {}
 
-        def quantise_low(t, a):
-            nc.vector.quantize_mx(
-                out=low_codes[t][:, a * P : (a + 1) * P].bitcast(FP8X4),
-                scales=low_planes[t][:, a * P : (a + 1) * P],
-                in_=low_bf[t, a][:],
-            )
-
-        def quantise_high(a):
-            nc.vector.quantize_mx(out=high_codes[a][:].bitcast(FP8X4), scales=high_planes[a][:], in_=high_bf[a][:])
-
-        def product(t, banks, stationary):
-            accs = [psum.tile([P, BANK], F32, name=banks) for u in range(S // BANK)]
+        def gate_sums(slices, first_bank):
+            halves = [(t, u) for u in range(2) for t in slices]
+            for t, u in halves:
+                sums[t, u] = bank(first_bank + 2 * (t - slices[0]) + u)
             for a in range(PASSES):
-                codes, scales = stationary(a, t)
-                for u, acc in enumerate(accs):
-                    nc.tensor.matmul_mx(
-                        out=acc[:],
-                        lhsT=codes,
-                        lhsT_scale=scales,
-                        rhs=v_words[a][:, u * BANK : (u + 1) * BANK].bitcast(FP8X4),
-                        rhs_scale=planes[:, a * S + u * BANK : a * S + (u + 1) * BANK],
-                        start=(a == 0),
-                        stop=(a == LAST),
-                    )
-            return accs
+                for t, u in halves:
+                    col = a * H + t * P
+                    codes = wg_codes[:, 2 * col : 2 * (col + P)].bitcast(FP4X4)
+                    first_stage_pass(sums[t, u], a, u, codes, wg_planes[:, col : col + P], a == 0, a == LAST)
+            for t, u in halves:
+                gates[t, u] = sb("gate%d_%d" % (t, u), [P, BANK], F32)
+                nc.scalar.activation(gates[t, u][:], sums[t, u][:], ACT.Sigmoid)
 
-        def wg_slice(a, t):
-            col = a * P if t < 2 else (2 * a + t - 2) * P
-            codes = wg_low[t] if t < 2 else wg_high
-            first = a * H + t * P
-            return codes[:, 2 * col : 2 * (col + P)].bitcast(FP4X4), wg_planes[:, first : first + P]
+        gate_sums([0, 1, 2], 0)
 
-        def w1_slice(a, t):
-            if t < 2:
-                return low_codes[t][:, a * P : (a + 1) * P].bitcast(FP8X4), low_planes[t][:, a * P : (a + 1) * P]
-            cols = slice((t - 2) * P, (t - 1) * P)
-            return high_codes[a][:, cols].bitcast(FP8X4), high_planes[a][:, cols]
+        w1_bf, w1_codes, w1_planes = {}, {}, {}
 
-        gates = {}
+        late_bf = sb("late_bf", [P, 4 * H], BF16)
 
-        def sigmoids(t, accs):
-            for u, acc in enumerate(accs):
-                name = "gate%d_%d" % (t, u)
-                if t < 2:
-                    gates[t, u] = placed(name, [P, BANK], F32, GATE1_AT + 4 * BANK * u if t else W1_AT[0, u])
-                else:
-                    gates[t, u] = in_turn(name, [P, BANK], F32, name)
-                nc.scalar.activation(gates[t, u][:], acc[:], ACT.Sigmoid)
-
-        w2_bf = {}
-        w2_planes = sb("w2_planes", [P, N], U8)
-
-        def round_w2(m0, m1, dest, copy):
+        def round_w1(a, t0, t1, copy):
+            if a > 0 and t0 == 2:
+                w1_bf[a, t0] = late_bf[:, (a - 1) * 2 * H : a * 2 * H]
+            else:
+                w1_bf[a, t0] = sb("w1_bf%d_%d" % (a, t0), [P, (t1 - t0) * H], BF16)[:]
             copy(
-                out=dest.rearrange("p (c i t) -> p c t i", i=4, t=PACK),
+                out=w1_bf[a, t0].rearrange("p (t g i j) -> p t g j i", t=t1 - t0, i=4, j=PACK),
+                in_=w1_raw[a][:].rearrange("p j (g t i) -> p t g j i", t=PACK, i=4)[:, t0:t1],
+            )
+
+        def quantise_w1(parts, rounded, tag=None):
+            codes = sb("w1_codes%d_%d" % parts[0], [P, len(parts) * P], U32, tag)
+            scales = sb("w1_planes%d_%d" % parts[0], [P, len(parts) * P], U8)
+            nc.vector.quantize_mx(out=codes[:].bitcast(FP8X4), scales=scales[:], in_=rounded)
+            for n, part in enumerate(parts):
+                cols = slice(n * P, (n + 1) * P)
+                w1_codes[part], w1_planes[part] = codes[:, cols].bitcast(FP8X4), scales[:, cols]
+
+        def content(t, first_bank, passes):
+            for u in range(2):
+                sums[t, u] = bank(first_bank + u)
+            for a in passes:
+                for u in range(2):
+                    first_stage_pass(sums[t, u], a, u, w1_codes[a, t], w1_planes[a, t], a == passes[0], a == passes[-1])
+
+        h = [sb("h%d" % t, [P, S], F32) for t in range(PACK)]
+
+        def make_h(t):
+            for u in range(2):
+                nc.vector.tensor_tensor(h[t][:, u * BANK : (u + 1) * BANK], sums[t, u][:], gates[t, u][:], MULT)
+
+        HOLD_AT = 6 * RAW
+        z = [sb("z0", [P, PACK * HALF], F32)]
+        z_codes = sb("z_codes", [P, PAIRS], U32)
+        z_planes = sb("z_planes", [P, PAIRS], U8)
+        w2_codes = sb("w2_codes", [P, N], U32)
+        w2_planes = sb("w2_planes", [P, N], U8)
+        w2_bf = {0: sb("w2_bf0", [P, 4 * P * PACK], BF16), 4: sb("w2_bf4", [P, 2 * P * PACK], BF16)}
+        factor = {}
+
+        def round_w2(m0, m1):
+            part = 0 if m0 < 4 else 4
+            nc.scalar.copy(
+                out=w2_bf[part][:, (m0 - part) * P * PACK : (m1 - part) * P * PACK].rearrange(
+                    "p (c i t) -> p c t i", i=4, t=PACK
+                ),
                 in_=w2_raw[:, :, m0 * P : m1 * P].rearrange("p t (c i) -> p c t i", i=4),
             )
 
         def quantise_w2(m0, m1):
             nc.vector.quantize_mx(
-                out=w2_codes[:, m0 * P : m1 * P].bitcast(FP8X4),
-                scales=w2_planes[:, m0 * P : m1 * P],
-                in_=w2_bf[m0][:],
+                out=w2_codes[:, m0 * P : m1 * P].bitcast(FP8X4), scales=w2_planes[:, m0 * P : m1 * P], in_=w2_bf[m0][:]
             )
 
-        h = [sb("h%d" % t, [P, S], F32) for t in range(PACK)]
-        z = [sb("z%d" % e, [P, PACK * HALF], F32) for e in range(2)]
-        z_codes = sb("z_codes", [P, PAIRS], U32)
-        z_planes = sb("z_planes", [P, PAIRS], U8)
+        def make_factor(t, j0, j1):
+            if (t, j0) == (3, HALF):
+                second = placed("second_back", [P, HALF], F32, HOLD_AT - 2 * HALF)
+            else:
+                second = sb("second%d_%d" % (t, j0), [P, j1 - j0], F32)
+            nc.vector.tensor_copy(second[:], h[t][:].indirect(pos2_sb[:, j0 // 16 : j1 // 16]))
+            if (t, j0) == (3, 0):
+                bent = placed("bent_front", [P, HALF], F32, HOLD_AT)
+            else:
+                bent = sb("bent%d_%d" % (t, j0), [P, j1 - j0], F32)
+            nc.scalar.activation(bent[:], second[:], ACT.Tanh)
+            made = sb("factor%d_%d" % (t, j0), [P, j1 - j0], F32)
+            nc.scalar.activation(made[:], bent[:], ACT.Copy, scale=gain_sb[t][:])
+            for j in range(j0, j1, QUARTER):
+                factor[t, j] = (made, j0)
 
-        def make_h(t, accs):
-            for u, acc in enumerate(accs):
-                cols = slice(u * BANK, (u + 1) * BANK)
-                nc.vector.tensor_tensor(h[t][:, cols], acc[:], gates[t, u][:], MULT)
+        def make_z(t, j0, j1):
+            made, base = factor[t, j0]
+            e = j0 // HALF
+            at = t * HALF + j0 - e * HALF
+            nc.vector.tensor_tensor(
+                z[e][:, at : at + j1 - j0],
+                h[t][:].indirect(pos1_sb[:, j0 // 16 : j1 // 16]),
+                made[:, j0 - base : j1 - base],
+                MULT,
+            )
 
-        def pick_second(t, j0, j1, dest):
-            nc.vector.tensor_copy(dest, h[t][:].indirect(pos2_sb[:, j0 // 16 : j1 // 16]))
-
-        def bend(t, j0, j1, second, dest):
-            nc.scalar.activation(dest, second, ACT.Tanh)
-
-        def pick_first(t, j0, j1, other, dest):
-            first = sb("first%d_%d" % (t, j0), [P, j1 - j0], F32)
-            nc.vector.tensor_copy(first[:], h[t][:].indirect(pos1_sb[:, j0 // 16 : j1 // 16]))
-            nc.vector.scalar_tensor_tensor(dest, first[:], gain_sb[t][:], other, MULT, MULT)
-
-        def move_low(t, z_low):
-            for e in range(2):
-                nc.sync.dma_start(
-                    out=z[e][64 * t : 64 * (t + 1), 0 : 2 * HALF].rearrange("p (s j) -> p s j", s=2),
-                    in_=z_low[:, e * HALF : (e + 1) * HALF],
-                )
-
-        def weave(j0, j1, z_bf, copy):
+        def weave(j0, j1, woven, copy):
             e = j0 // HALF
             copy(
-                out=z_bf.rearrange("p (c i t) -> p c t i", i=4, t=PACK),
+                out=woven.rearrange("p (c i t) -> p c t i", i=4, t=PACK),
                 in_=z[e][:].rearrange("p (t c i) -> p c t i", t=PACK, i=4)[:, (j0 - e * HALF) // 4 : (j1 - e * HALF) // 4],
             )
 
-        def quantise_z(j0, j1, z_bf):
-            nc.vector.quantize_mx(out=z_codes[:, j0:j1].bitcast(FP8X4), scales=z_planes[:, j0:j1], in_=z_bf)
+        def quantise_z(j0, j1, woven):
+            nc.vector.quantize_mx(out=z_codes[:, j0:j1].bitcast(FP8X4), scales=z_planes[:, j0:j1], in_=woven)
 
         def project(j0, j1, banks, copies):
             width = j1 - j0
             blocks = N // P // len(banks)
             for g, copy in enumerate(copies):
-                acc = psum.tile([P, BANK], F32, name=banks[g])
+                acc = bank(banks[g])
                 for s in range(blocks):
                     m = blocks * g + s
                     nc.tensor.matmul_mx(
@@ -306,101 +287,54 @@ def tile_list_fused_passage_pairs_kernel(
                 )
 
         on_scalar, on_vector = nc.scalar.copy, nc.vector.tensor_copy
-        gather_words(LAST, 0, BANK)
-        gather_words(LAST, BANK, S)
-        gain_sb = [placed("gain%d" % t, [P, 1], F32, TABLE_AT[LAST] + 64 * t) for t in range(PACK)]
-        gain_low = gain.rearrange("(t b g j o) -> g t b j o", t=2, g=2, j=8, o=1)[0]
-        gain_high = gain.rearrange("(b g t i o) -> g t b i o", g=2, t=2, i=4, o=1)[1]
-        with nc.allow_non_contiguous_dma(reason="one gain to a partition"):
-            for t in range(PACK):
-                nc.sync.dma_start(out=gain_sb[t][:], in_=(gain_low if t < 2 else gain_high)[t % 2])
-        w2_raw = placed("w2_raw", [P, PACK, N], F32, TABLE_AT[LAST] + 64 * PACK)
-        nc.sync.dma_start(
-            out=w2_raw[:, 0:2, :].rearrange("p t n -> p (t n)"),
-            in_=w2.rearrange("(b g i t) n -> g b i (t n)", g=2, i=4, t=2)[0],
-        )
-        w2_high = w2.rearrange("(b g t i) n -> g t b i n", g=2, t=2, i=4)[1]
+        round_w1(0, 0, PACK, on_vector)
+        quantise_w1([(0, t) for t in range(PACK)], w1_bf[0, 0])
+        round_w1(1, 0, 2, on_vector)
+        quantise_w1([(1, 0), (1, 1)], w1_bf[1, 0])
+        round_w1(1, 2, PACK, on_scalar)
+        round_w1(LAST, 0, 1, on_vector)
+        round_w1(LAST, 1, 2, on_vector)
+        round_w1(LAST, 2, PACK, on_scalar)
         for t in range(2):
-            nc.sync.dma_start(out=w2_raw[:, 2 + t, :], in_=w2_high[t])
-        for a in range(PASSES):
-            round_low(0, a, on_vector if a == LAST else on_scalar)
-            quantise_low(0, a)
-            if a < LAST:
-                round_high(0, a, on_scalar)
-        round_high(0, LAST, on_vector)
-        gate_sums = product(0, "acc_a", wg_slice)
-        sigmoids(0, gate_sums)
-        make_h(0, product(0, "acc_x", w1_slice))
-        deal_wg(1)
-        second = {}
-        for a in range(PASSES):
-            round_low(1, a, on_scalar)
-            quantise_low(1, a)
-        second[0] = in_turn("second0", [P, PAIRS], F32, "low_bf1_0")
-        pick_second(0, 0, PAIRS, second[0][:])
-        sigmoids(1, product(1, "acc_y", wg_slice))
-        make_h(1, product(1, "acc_b", w1_slice))
-        for a in range(PASSES):
-            round_high(1, a, on_scalar)
-            quantise_high(a)
-        second[1] = in_turn("second1", [P, PAIRS], F32, "low_bf0_%d" % LAST)
-        pick_second(1, 0, PAIRS, second[1][:])
-        factor = [placed("factor0", [P, PAIRS], F32, GATE1_AT), sb("factor1", [P, PAIRS], F32)]
-        bend(0, 0, PAIRS, second[0][:], factor[0][:])
-        z_low = [sb("z_low0", [P, PAIRS], F32)]
-        pick_first(0, 0, PAIRS, factor[0][:], z_low[0][:])
-        move_low(0, z_low[0])
-        sigmoids(2, product(2, "acc_y", wg_slice))
-        make_h(2, product(2, "acc_b", w1_slice))
-        bend(1, 0, PAIRS, second[1][:], factor[1][:])
-        second[2] = sb("second2", [P, PAIRS], F32)
-        pick_second(2, 0, PAIRS, second[2][:])
-        z_low.append(in_turn("z_low1", [P, PAIRS], F32, "gate2_1"))
-        pick_first(1, 0, PAIRS, factor[1][:], z_low[1][:])
-        move_low(1, z_low[1])
-        sigmoids(3, product(3, "acc_y", wg_slice))
-        make_h(3, product(3, "acc_b", w1_slice))
-        w2_bf[0] = sb("w2_bf0", [P, 4 * P * PACK], BF16)
-        for m in range(4):
-            round_w2(m, m + 1, w2_bf[0][:, m * P * PACK : (m + 1) * P * PACK], on_scalar)
-
-        END = GATE1_AT + 8 * BANK
-        front_factor = [
-            in_turn("front_factor0", [P, HALF], F32, "after_front0"),
-            placed("front_factor1", [P, HALF], F32, END + 2 * HALF),
-        ]
-        back_factor = [sb("back_factor%d" % t, [P, HALF], F32) for t in range(2)]
-        last_second = sb("last_second", [P, HALF], F32)
-        bend(2, 0, HALF, second[2][:, 0:HALF], front_factor[0][:])
-        pick_second(3, 0, HALF, last_second[:])
-        bend(3, 0, HALF, last_second[:], front_factor[1][:])
-        for t in range(2):
-            pick_first(2 + t, 0, HALF, front_factor[t][:], z[0][:, (2 + t) * HALF : (3 + t) * HALF])
-        w2_bf[4] = sb("w2_bf4", [P, 2 * P * PACK], BF16)
-        round_w2(4, 6, w2_bf[4][:], on_scalar)
-        z_bf_front = z[1][:, 2 * HALF :].bitcast(BF16)
-        weave(0, HALF, z_bf_front, on_scalar)
-        back_second = placed("back_second", [P, HALF], F32, END)
-        pick_second(3, HALF, PAIRS, back_second[:])
-        w2_codes = placed("w2_codes", [P, N], U32, END + 4 * HALF)
+            quantise_w1([(LAST, t)], w1_bf[LAST, t])
+        content(0, 6, [0, 1, 2])
+        content(1, 0, [0, 1, 2])
+        make_h(0)
+        quantise_w1([(a, t) for a in range(1, PASSES) for t in range(2, PACK)], late_bf[:], "gate0_0")
+        gate_sums([3], 6)
+        content(2, 2, [1, 2, 0])
+        content(3, 4, [1, 2, 0])
+        make_h(1)
+        make_factor(0, 0, PAIRS)
+        make_factor(1, 0, PAIRS)
+        make_h(2)
+        make_z(0, 0, HALF)
+        make_h(3)
+        make_z(1, 0, HALF)
+        for m in range(0, N // P, 2):
+            round_w2(m, m + 2)
+        make_factor(2, 0, PAIRS)
+        make_factor(3, 0, HALF)
         quantise_w2(0, 4)
         quantise_w2(4, 6)
-        bend(2, HALF, PAIRS, second[2][:, HALF:], back_factor[0][:])
-        bend(3, HALF, PAIRS, back_second[:], back_factor[1][:])
-        quantise_z(0, HALF, z_bf_front)
-        project(0, HALF, ["acc_x", "acc_a", "acc_x"], [on_scalar] * 3)
-        QUARTER = HALF // 2
-        pick_first(2, HALF, PAIRS, back_factor[0][:], z[1][:, 2 * HALF : 3 * HALF])
-        woven = [sb("woven%d" % c, [P, QUARTER * PACK], BF16) for c in range(2)]
-        for c in range(2):
-            j0 = HALF + c * QUARTER
-            cols = slice(c * QUARTER, (c + 1) * QUARTER)
-            pick_first(3, j0, j0 + QUARTER, back_factor[1][:, cols], z[1][:, 3 * HALF :][:, cols])
-        for c in range(2):
-            j0 = HALF + c * QUARTER
-            weave(j0, j0 + QUARTER, woven[c][:], on_vector)
-        for c in range(2):
-            j0 = HALF + c * QUARTER
-            quantise_z(j0, j0 + QUARTER, woven[c][:])
-        project(HALF, HALF + QUARTER, ["acc_a", "acc_y"], [on_vector, on_scalar])
-        project(HALF + QUARTER, PAIRS, ["acc_b", "acc_y"], [on_vector, on_scalar])
+        make_z(2, 0, HALF)
+        make_z(3, 0, HALF)
+        z.append(placed("z1", [P, PACK * HALF], F32, HOLD_AT + 2 * HALF))
+        front = z[1][:, 2 * HALF :].bitcast(BF16)
+        weave(0, HALF, front, on_scalar)
+        make_factor(3, HALF, PAIRS)
+        make_z(0, HALF, PAIRS)
+        make_z(1, HALF, PAIRS)
+        quantise_z(0, HALF, front)
+        project(0, HALF, [0, 1, 2], [on_scalar] * 3)
+        make_z(2, HALF, PAIRS)
+        quarters = [HALF, HALF + QUARTER]
+        for j in quarters:
+            make_z(3, j, j + QUARTER)
+        woven = {j: sb("woven%d" % j, [P, QUARTER * PACK], BF16) for j in quarters}
+        for j in quarters:
+            weave(j, j + QUARTER, woven[j][:], on_vector)
+        for j in quarters:
+            quantise_z(j, j + QUARTER, woven[j][:])
+        project(HALF, HALF + QUARTER, [3, 4], [on_vector, on_scalar])
+        project(HALF + QUARTER, PAIRS, [5, 6], [on_vector, on_scalar])

@@ -193,8 +193,8 @@ def tile_list_fused_passage_pairs_kernel(
         def content(t, first_bank, passes):
             for u in range(2):
                 sums[t, u] = bank(first_bank + u)
-            for a in passes:
-                for u in range(2):
+            for u in range(2):
+                for a in passes:
                     first_stage_pass(sums[t, u], a, u, w1_codes[a, t], w1_planes[a, t], a == passes[0], a == passes[-1])
 
         h = [sb("h%d" % t, [P, S], F32) for t in range(PACK)]
@@ -298,7 +298,7 @@ def tile_list_fused_passage_pairs_kernel(
         for t in range(2):
             quantise_w1([(LAST, t)], w1_bf[LAST, t])
         content(0, 6, [0, 1, 2])
-        content(1, 0, [0, 1, 2])
+        content(1, 0, [0, 2, 1])
         make_h(0)
         quantise_w1([(a, t) for a in range(1, PASSES) for t in range(2, PACK)], late_bf[:], "gate0_0")
         gate_sums([3], 6)

from contextlib import ExitStack

import concourse.mybir as mybir

K, T, S, PAIRS, H, N = 1536, 2048, 1024, 512, 512, 768
FLOPS = 2 * (2 * K * H * S + H * N * PAIRS)

F32 = mybir.dt.float32
BF16 = mybir.dt.bfloat16
I32 = mybir.dt.int32
U32 = mybir.dt.uint32
U16 = mybir.dt.uint16
U8 = mybir.dt.uint8
FP8X4 = mybir.dt.float8_e4m3fn_x4
FP4X4 = mybir.dt.float4_e2m1fn_x4
MULT = mybir.AluOpType.mult
ACT = mybir.ActivationFunctionType

P = 128
PACK = 4
PASSES = K // (P * PACK)
LAST = PASSES - 1
BANK = 512
HALF = PAIRS // 2
QUARTER = PAIRS // 4
SCALE_ROWS = 16 * PASSES
ROW0 = 48


def tile_list_fused_passage_pairs_kernel(
    tc, tab_words, tab_scales, offs, pos1, pos2, w1, wg_words, wg_scales, gain, w2, out
):
    nc = tc.nc
    with ExitStack() as ctx:
        keep = ctx.enter_context(tc.tile_pool(name="keep", bufs=1))
        shared = ctx.enter_context(tc.tile_pool(name="shared", bufs=1))
        psum = ctx.enter_context(tc.psum_pool(name="psum", bufs=1))

        def sb(name, shape, dtype, tag=None):
            return keep.tile(shape, dtype, name=name, tag=tag or name, align_bytes=64)

        def placed(name, shape, dtype, offset):
            return shared.tile(shape, dtype, name=name, offset=offset, align_bytes=64)

        def bank(number):
            return psum.tile([P, BANK], F32, name="bank%d" % number)

        offs_sb = keep.tile([P, S // 16], U16, name="offs_sb")
        pos1_sb = keep.tile([P, PAIRS // 16], U16, name="pos1_sb")
        pos2_sb = keep.tile([P, PAIRS // 16], U16, name="pos2_sb")

        RAW = 4 * PACK * H
        TABLE_AT = [RAW // 2, 2 * RAW, 3 * RAW]
        scale_rows = placed("scale_rows", [P, T], U8, TABLE_AT[LAST])
        wg_scale_rows = sb("wg_scale_rows", [P, PASSES * H], U8)
        planes = sb("planes", [P, PASSES * S], U8)

        nc.sync.dma_start(offs_sb[:], offs)
        for a in range(PASSES):
            rows = scale_rows[ROW0 + a : ROW0 + 32 : 2, :] if a < LAST else scale_rows[ROW0 + 32 : ROW0 + SCALE_ROWS, :]
            nc.sync.dma_start(out=rows.bitcast(I32), in_=tab_scales.bitcast(I32)[a])
        nc.vector.memset(scale_rows[0:ROW0, :].bitcast(I32), 0)
        nc.vector.memset(scale_rows[ROW0 + SCALE_ROWS :, :].bitcast(I32), 0)
        nc.vector.memset(wg_scale_rows[:].bitcast(I32), 0)
        nc.vector.memset(planes[:].bitcast(I32), 0)

        warm = sb("warm", [P, 2], F32)
        nc.vector.memset(warm[:, 0:1], 0.0)
        nc.scalar.activation(warm[:, 1:2], warm[:, 0:1], ACT.Sigmoid)

        table = {}

        def load_table(a):
            table[a] = placed("table%d" % a, [P, T], U32, TABLE_AT[a])
            nc.sync.dma_start(
                out=table[a][:].bitcast(I32),
                in_=tab_words[a].rearrange("p t i -> p (t i)").bitcast(I32),
            )

        w1_raw = {}

        def load_w1(a):
            w1_raw[a] = placed("w1_raw%d" % a, [P, PACK, H], F32, a * RAW)
            nc.sync.dma_start(out=w1_raw[a][:], in_=w1[512 * a : 512 * (a + 1), :].rearrange("(p j) c -> p j c", j=PACK))

        load_table(0)
        for q in range(4):
            nc.sync.dma_start(
                out=wg_scale_rows[32 * q : 32 * q + 4, :].bitcast(I32).rearrange("r (a c) -> r a c", a=PASSES),
                in_=wg_scales.bitcast(I32)[:, 4 * q : 4 * q + 4, :].rearrange("a r c -> r a c"),
            )
        wg_raw = sb("wg_raw", [P, PASSES, H // 2], I32)
        nc.sync.dma_start(out=wg_raw[:], in_=wg_words.bitcast(I32).rearrange("a p e -> p a e"))
        load_table(1)
        nc.sync.dma_start(pos2_sb[:], pos2)
        nc.sync.dma_start(pos1_sb[:], pos1)

        picked_rows = sb("picked_rows", [P, S], U8)
        nc.vector.tensor_copy(picked_rows[:], scale_rows[:].indirect(offs_sb[:]))
        for q in range(4):
            nc.sync.dma_start(
                out=planes[32 * q : 32 * q + 4, 0 : 2 * S].bitcast(I32).rearrange("r (a s) -> r a s", a=2),
                in_=picked_rows[ROW0 + 8 * q : ROW0 + 8 * q + 8, :].bitcast(I32),
            )
        load_table(LAST)
        for q in range(4):
            nc.sync.dma_start(
                out=planes[32 * q : 32 * q + 4, 2 * S :].bitcast(I32),
                in_=picked_rows[ROW0 + 32 + 4 * q : ROW0 + 32 + 4 * q + 4, :].bitcast(I32),
            )

        wg_planes = sb("wg_planes", [P, PASSES * H], U8)
        nc.scalar.copy(
            out=wg_planes[:].bitcast(U32).rearrange("p (a t g) -> p a t g", a=PASSES, t=PACK),
            in_=wg_scale_rows[:].bitcast(U32).rearrange("p (a g t) -> p a t g", a=PASSES, t=PACK),
        )
        wg_codes = sb("wg_codes", [P, PASSES * 2 * H], U8)
        nc.scalar.copy(
            out=wg_codes[:].bitcast(U32).rearrange("p (a t g w) -> p a t g w", a=PASSES, t=PACK, w=2),
            in_=wg_raw[:].bitcast(U32).rearrange("p a (g t w) -> p a t g w", t=PACK, w=2),
        )

        v_words = [sb("v_words%d" % a, [P, S], U32) for a in range(PASSES)]

        def gather_words(a, s0, s1):
            nc.vector.tensor_copy(v_words[a][:, s0:s1], table[a][:].indirect(offs_sb[:, s0 // 16 : s1 // 16]))

        gather_words(0, 0, S)
        load_w1(0)
        load_w1(1)
        gather_words(1, 0, S)
        load_w1(LAST)
        gather_words(LAST, 0, BANK)
        gather_words(LAST, BANK, S)
        gain_sb = [placed("gain%d" % t, [P, 1], F32, TABLE_AT[LAST] + 64 * t) for t in range(PACK)]
        with nc.allow_non_contiguous_dma(reason="one gain to a partition"):
            for t in range(PACK):
                nc.sync.dma_start(out=gain_sb[t][:], in_=gain.rearrange("(g t i o) -> t g i o", t=PACK, i=4, o=1)[t])
        w2_raw = placed("w2_raw", [P, PACK, N], F32, TABLE_AT[LAST] + 64 * PACK)
        for t in range(PACK):
            nc.sync.dma_start(out=w2_raw[:, t, :], in_=w2.rearrange("(g t i) n -> t g i n", t=PACK, i=4)[t])

        def first_stage_pass(acc, a, u, codes, scales, start, stop):
            nc.tensor.matmul_mx(
                out=acc[:],
                lhsT=codes,
                lhsT_scale=scales,
                rhs=v_words[a][:, u * BANK : (u + 1) * BANK].bitcast(FP8X4),
                rhs_scale=planes[:, a * S + u * BANK : a * S + (u + 1) * BANK],
                start=start,
                stop=stop,
            )

        sums, gates = {}, {}

        def gate_sums(slices, first_bank):
            halves = [(t, u) for u in range(2) for t in slices]
            for t, u in halves:
                sums[t, u] = bank(first_bank + 2 * (t - slices[0]) + u)
            for a in range(PASSES):
                for t, u in halves:
                    col = a * H + t * P
                    codes = wg_codes[:, 2 * col : 2 * (col + P)].bitcast(FP4X4)
                    first_stage_pass(sums[t, u], a, u, codes, wg_planes[:, col : col + P], a == 0, a == LAST)
            for t, u in halves:
                gates[t, u] = sb("gate%d_%d" % (t, u), [P, BANK], F32)
                nc.scalar.activation(gates[t, u][:], sums[t, u][:], ACT.Sigmoid)

        gate_sums([0, 1, 2], 0)

        w1_bf, w1_codes, w1_planes = {}, {}, {}

        late_bf = sb("late_bf", [P, 4 * H], BF16)

        def round_w1(a, t0, t1, copy):
            if a > 0 and t0 == 2:
                w1_bf[a, t0] = late_bf[:, (a - 1) * 2 * H : a * 2 * H]
            else:
                w1_bf[a, t0] = sb("w1_bf%d_%d" % (a, t0), [P, (t1 - t0) * H], BF16)[:]
            copy(
                out=w1_bf[a, t0].rearrange("p (t g i j) -> p t g j i", t=t1 - t0, i=4, j=PACK),
                in_=w1_raw[a][:].rearrange("p j (g t i) -> p t g j i", t=PACK, i=4)[:, t0:t1],
            )

        def quantise_w1(parts, rounded, tag=None):
            codes = sb("w1_codes%d_%d" % parts[0], [P, len(parts) * P], U32, tag)
            scales = sb("w1_planes%d_%d" % parts[0], [P, len(parts) * P], U8)
            nc.vector.quantize_mx(out=codes[:].bitcast(FP8X4), scales=scales[:], in_=rounded)
            for n, part in enumerate(parts):
                cols = slice(n * P, (n + 1) * P)
                w1_codes[part], w1_planes[part] = codes[:, cols].bitcast(FP8X4), scales[:, cols]

        def content(t, first_bank, passes):
            for u in range(2):
                sums[t, u] = bank(first_bank + u)
            for u in range(2):
                for a in passes:
                    first_stage_pass(sums[t, u], a, u, w1_codes[a, t], w1_planes[a, t], a == passes[0], a == passes[-1])

        h = [sb("h%d" % t, [P, S], F32) for t in range(PACK)]

        def make_h(t):
            for u in range(2):
                nc.vector.tensor_tensor(h[t][:, u * BANK : (u + 1) * BANK], sums[t, u][:], gates[t, u][:], MULT)

        HOLD_AT = 6 * RAW
        z = [sb("z0", [P, PACK * HALF], F32)]
        z_codes = sb("z_codes", [P, PAIRS], U32)
        z_planes = sb("z_planes", [P, PAIRS], U8)
        w2_codes = sb("w2_codes", [P, N], U32)
        w2_planes = sb("w2_planes", [P, N], U8)
        w2_bf = {0: sb("w2_bf0", [P, 4 * P * PACK], BF16), 4: sb("w2_bf4", [P, 2 * P * PACK], BF16)}
        factor = {}

        def round_w2(m0, m1):
            part = 0 if m0 < 4 else 4
            nc.scalar.copy(
                out=w2_bf[part][:, (m0 - part) * P * PACK : (m1 - part) * P * PACK].rearrange(
                    "p (c i t) -> p c t i", i=4, t=PACK
                ),
                in_=w2_raw[:, :, m0 * P : m1 * P].rearrange("p t (c i) -> p c t i", i=4),
            )

        def quantise_w2(m0, m1):
            nc.vector.quantize_mx(
                out=w2_codes[:, m0 * P : m1 * P].bitcast(FP8X4), scales=w2_planes[:, m0 * P : m1 * P], in_=w2_bf[m0][:]
            )

        def make_factor(t, j0, j1):
            if (t, j0) == (3, HALF):
                second = placed("second_back", [P, HALF], F32, HOLD_AT - 2 * HALF)
            else:
                second = sb("second%d_%d" % (t, j0), [P, j1 - j0], F32)
            nc.vector.tensor_copy(second[:], h[t][:].indirect(pos2_sb[:, j0 // 16 : j1 // 16]))
            if (t, j0) == (3, 0):
                bent = placed("bent_front", [P, HALF], F32, HOLD_AT)
            else:
                bent = sb("bent%d_%d" % (t, j0), [P, j1 - j0], F32)
            nc.scalar.activation(bent[:], second[:], ACT.Tanh)
            made = sb("factor%d_%d" % (t, j0), [P, j1 - j0], F32)
            nc.scalar.activation(made[:], bent[:], ACT.Copy, scale=gain_sb[t][:])
            for j in range(j0, j1, QUARTER):
                factor[t, j] = (made, j0)

        def make_z(t, j0, j1):
            made, base = factor[t, j0]
            e = j0 // HALF
            at = t * HALF + j0 - e * HALF
            nc.vector.tensor_tensor(
                z[e][:, at : at + j1 - j0],
                h[t][:].indirect(pos1_sb[:, j0 // 16 : j1 // 16]),
                made[:, j0 - base : j1 - base],
                MULT,
            )

        def weave(j0, j1, woven, copy):
            e = j0 // HALF
            copy(
                out=woven.rearrange("p (c i t) -> p c t i", i=4, t=PACK),
                in_=z[e][:].rearrange("p (t c i) -> p c t i", t=PACK, i=4)[:, (j0 - e * HALF) // 4 : (j1 - e * HALF) // 4],
            )

        def quantise_z(j0, j1, woven):
            nc.vector.quantize_mx(out=z_codes[:, j0:j1].bitcast(FP8X4), scales=z_planes[:, j0:j1], in_=woven)

        def project(j0, j1, banks, copies):
            width = j1 - j0
            blocks = N // P // len(banks)
            for g, copy in enumerate(copies):
                acc = bank(banks[g])
                for s in range(blocks):
                    m = blocks * g + s
                    nc.tensor.matmul_mx(
                        out=acc[:, s * width : (s + 1) * width],
                        lhsT=w2_codes[:, m * P : (m + 1) * P].bitcast(FP8X4),
                        lhsT_scale=w2_planes[:, m * P : (m + 1) * P],
                        rhs=z_codes[:, j0:j1].bitcast(FP8X4),
                        rhs_scale=z_planes[:, j0:j1],
                        start=True,
                        stop=True,
                    )
                res = sb("res%d_%d" % (j0, g), [P, blocks * width], F32)
                copy(out=res[:], in_=acc[:, 0 : blocks * width])
                nc.sync.dma_start(
                    out=out[blocks * g * P : blocks * (g + 1) * P, j0:j1].rearrange("(s p) j -> p s j", p=P),
                    in_=res[:].rearrange("p (s j) -> p s j", s=blocks),
                )

        on_scalar, on_vector = nc.scalar.copy, nc.vector.tensor_copy
        round_w1(0, 0, PACK, on_vector)
        quantise_w1([(0, t) for t in range(PACK)], w1_bf[0, 0])
        round_w1(1, 0, 2, on_vector)
        quantise_w1([(1, 0), (1, 1)], w1_bf[1, 0])
        round_w1(1, 2, PACK, on_scalar)
        round_w1(LAST, 0, 1, on_vector)
        round_w1(LAST, 1, 2, on_vector)
        round_w1(LAST, 2, PACK, on_scalar)
        for t in range(2):
            quantise_w1([(LAST, t)], w1_bf[LAST, t])
        content(0, 6, [0, 1, 2])
        content(1, 0, [0, 2, 1])
        make_h(0)
        quantise_w1([(a, t) for a in range(1, PASSES) for t in range(2, PACK)], late_bf[:], "gate0_0")
        gate_sums([3], 6)
        content(2, 2, [1, 2, 0])
        content(3, 4, [1, 2, 0])
        make_h(1)
        make_factor(0, 0, PAIRS)
        make_factor(1, 0, PAIRS)
        make_h(2)
        make_z(0, 0, HALF)
        make_h(3)
        make_z(1, 0, HALF)
        for m in range(0, N // P, 2):
            round_w2(m, m + 2)
        make_factor(2, 0, PAIRS)
        make_factor(3, 0, HALF)
        quantise_w2(0, 4)
        quantise_w2(4, 6)
        make_z(2, 0, HALF)
        make_z(3, 0, HALF)
        z.append(placed("z1", [P, PACK * HALF], F32, HOLD_AT + 2 * HALF))
        front = z[1][:, 2 * HALF :].bitcast(BF16)
        weave(0, HALF, front, on_scalar)
        make_factor(3, HALF, PAIRS)
        make_z(0, HALF, PAIRS)
        make_z(1, HALF, PAIRS)
        quantise_z(0, HALF, front)
        project(0, HALF, [0, 1, 2], [on_scalar] * 3)
        make_z(2, HALF, PAIRS)
        quarters = [HALF, HALF + QUARTER]
        for j in quarters:
            make_z(3, j, j + QUARTER)
        woven = {j: sb("woven%d" % j, [P, QUARTER * PACK], BF16) for j in quarters}
        for j in quarters:
            weave(j, j + QUARTER, woven[j][:], on_vector)
        for j in quarters:
            quantise_z(j, j + QUARTER, woven[j][:])
        project(HALF, HALF + QUARTER, [3, 4], [on_vector, on_scalar])
        project(HALF + QUARTER, PAIRS, [5, 6], [on_vector, on_scalar])
